import numpy as np
import ml_dtypes


def mxq(x, axis, fmt="e4m3"):
    dtype, down = {"e4m3": (ml_dtypes.float8_e4m3fn, 7), "e5m2": (ml_dtypes.float8_e5m2, 14)}[fmt]
    v = np.moveaxis(np.asarray(x, np.float32).astype(ml_dtypes.bfloat16).astype(np.float64), axis, -1)
    blocks = v.reshape(v.shape[:-1] + (-1, 32))
    amax = np.abs(blocks).max(-1, keepdims=True)
    byte = np.maximum(np.where(amax > 0, np.frexp(amax)[1] - 1 + 127, 0) - down, 1)
    scale = np.exp2(byte - 127.0)
    codes = (blocks / scale).astype(np.float32).astype(dtype).astype(np.float64)
    return np.moveaxis((codes * scale).reshape(v.shape), -1, axis)


WIDE = False


def mx_kscale(k):
    if not WIDE:
        return np.ones(k)
    levels = np.array([10, -10, 5, -5, 0])
    if k % 512:
        return np.exp2(np.random.permutation(np.resize(levels, k // 32))).repeat(32)
    a = np.empty((k // 512, 16))
    for p in range(k // 512):
        a[p, :8] = np.random.permutation(np.resize(levels, 8))
        for g in range(8):
            far = levels[np.abs(levels - a[p, g]) >= 10]
            a[p, g + 8] = far[np.random.randint(len(far))]
    return np.exp2(a.ravel()).repeat(32)


def f64(x):
    return np.asarray(x).astype(np.float64)


def striped(idx):
    return np.tile(idx.reshape(-1, 16).T, (8, 1)).astype(np.uint16)


def unstriped(offs):
    return offs[:16].T.reshape(-1).astype(np.int64)


E2M1 = np.array([0.0, 0.5, 1.0, 1.5, 2.0, 3.0, 4.0, 6.0, -0.0, -0.5, -1.0, -1.5, -2.0, -3.0, -4.0, -6.0])


def pack_weight(w, fmt):
    k, n = w.shape
    w = f64(np.asarray(w, np.float32).astype(ml_dtypes.bfloat16)).reshape(k // 32, 32, n)
    amax = np.abs(w).max(1)
    if fmt == "e4m3":
        byte = np.frexp(amax)[1] - 1 + 127 - 7
    else:
        mant, ex = np.frexp(amax / 6.0)
        byte = np.where(mant > 0.5, ex, ex - 1) + 127
    byte = np.clip(np.where(amax > 0, byte, 1), 1, 254)
    scaled = (w * np.exp2(127.0 - byte)[:, None, :]).reshape(k, n).astype(np.float32)
    by_word = np.ascontiguousarray(scaled.reshape(k // 512, 128, 4, n).transpose(0, 1, 3, 2))
    if fmt == "e4m3":
        words = by_word.astype(ml_dtypes.float8_e4m3fn).view(np.uint8)
    else:
        c = by_word.astype(ml_dtypes.float4_e2m1fn).view(np.uint8) & 0xF
        words = (c[..., 0::2] | (c[..., 1::2] << 4)).reshape(k // 512, 128, 2 * n)
    return np.ascontiguousarray(words), np.ascontiguousarray(byte.astype(np.uint8).reshape(k // 512, 16, n))


def unpack_weight(words, scales, fmt):
    g, _, n = scales.shape
    words = np.ascontiguousarray(words).reshape(g, 128, n, -1)
    if fmt == "e4m3":
        vals = words.view(ml_dtypes.float8_e4m3fn).astype(np.float64)
    else:
        nib = np.empty((g, 128, n, 4), np.uint8)
        nib[..., 0::2] = words & 0xF
        nib[..., 1::2] = words >> 4
        vals = E2M1[nib]
    vals = vals * np.repeat(np.exp2(scales.astype(np.float64) - 127.0), 8, axis=1)[..., None]
    return vals.transpose(0, 1, 3, 2).reshape(g * 512, n)


def silu(v):
    return v / (1.0 + np.exp(-np.maximum(v, -700.0)))


K, T, E, C, H, N = 512, 2048, 8, 128, 512, 384


def by_expert(wq, xq):
    return np.concatenate([wq[e].T @ xq[:, e * C:(e + 1) * C] for e in range(E)], axis=1)


def setup_inputs():
    n = np.random.standard_normal
    s = mx_kscale(K)[:, None]
    u = mx_kscale(H)
    w1 = [pack_weight(m, "e2m1") for m in n((E, K, H)) / np.sqrt(K) / s[None]]
    w3 = [pack_weight(m, "e2m1") for m in n((E, K, H)) / np.sqrt(K) / s[None] * u[None, None, :]]
    w2 = [pack_weight(m, "e2m1") for m in n((E, H, N)) / np.sqrt(H) / u[None, :, None]]
    x = pack_weight(n((K, T)) * s, "e4m3")
    return {
        "x_words": x[0],
        "x_scales": x[1],
        "w1_words": np.stack([m[0] for m in w1]),
        "w1_scales": np.stack([m[1] for m in w1]),
        "w3_words": np.stack([m[0] for m in w3]),
        "w3_scales": np.stack([m[1] for m in w3]),
        "w2_words": np.stack([m[0] for m in w2]),
        "w2_scales": np.stack([m[1] for m in w2]),
        "gate": np.tile(np.random.uniform(0.2, 1.0, E * C), (N, 1)).astype(np.float32),
        "offs": striped(np.random.permutation(T)[:E * C]),
    }


def reference(x_words, x_scales, w1_words, w1_scales, w3_words, w3_scales, w2_words, w2_scales, gate, offs):
    idx = unstriped(offs)
    w1 = np.stack([unpack_weight(w1_words[e], w1_scales[e], "e2m1") for e in range(E)])
    w3 = np.stack([unpack_weight(w3_words[e], w3_scales[e], "e2m1") for e in range(E)])
    w2 = np.stack([unpack_weight(w2_words[e], w2_scales[e], "e2m1") for e in range(E)])
    xq = unpack_weight(x_words, x_scales, "e4m3")[:, idx]
    h = silu(by_expert(w1, xq))
    h = h * by_expert(w3, xq)
    y = by_expert(w2, mxq(h, 0, "e4m3"))
    out = np.zeros((N, T))
    out[:, idx] = f64(gate) * y
    return out

@@ -1,0 +1,187 @@
+from contextlib import ExitStack
+
+import concourse.mybir as mybir
+from concourse.masks import make_identity
+
+K, T, E, C, H, N = 512, 2048, 8, 128, 512, 384
+S = E * C
+P = 128
+FLOPS = 2 * S * (2 * K * H + H * N)
+
+F32 = mybir.dt.float32
+BF16 = mybir.dt.bfloat16
+I32 = mybir.dt.int32
+U32 = mybir.dt.uint32
+U16 = mybir.dt.uint16
+U8 = mybir.dt.uint8
+FP8X4 = mybir.dt.float8_e4m3fn_x4
+FP4X4 = mybir.dt.float4_e2m1fn_x4
+MULT = mybir.AluOpType.mult
+SILU = mybir.ActivationFunctionType.Silu
+
+GROUPS = ((0, 2), (2, 4), (4, 8))
+WORD_GATHERS = ((0, 2), (2, 8))
+
+
+def tile_moe_pkd_glu_silu_kernel(
+    tc, x_words, x_scales, w1_words, w1_scales, w3_words, w3_scales, w2_words, w2_scales, gate, offs, out
+):
+    nc = tc.nc
+    with ExitStack() as ctx:
+        keep = ctx.enter_context(tc.tile_pool(name="keep", bufs=1))
+        ring = ctx.enter_context(tc.tile_pool(name="ring", bufs=3))
+        psum = ctx.enter_context(tc.psum_pool(name="psum", bufs=1))
+
+        def held(shape, dtype, name):
+            return keep.tile(shape, dtype, name=name, align_bytes=64)
+
+        offsets = keep.tile([P, S // 16], U16, name="offsets")
+        nc.sync.dma_start(offsets[:], offs)
+
+        def slots(first, last):
+            return offsets[:, first * C // 16 : last * C // 16]
+
+        def load_scales(queue, scales, name):
+            experts, width = scales.shape[1], scales.shape[2]
+            plane = held([P, experts * width], U8, name)
+            words = plane[:].bitcast(I32)
+            nc.vector.memset(words, 0)
+            rows = scales.rearrange("(q r) e w -> r q e w", r=4)
+            for r in range(4):
+                queue.dma_start(
+                    words[r:P:32, :].rearrange("q (e w) -> q e w", e=experts), rows[r].bitcast(I32)
+                )
+            return plane
+
+        def load_words(words, first, last, name):
+            width = words.shape[3]
+            tile = held([P, last - first, width], U8, name)
+            nc.sync.dma_start(
+                tile[:].bitcast(I32), words[first:last, 0].rearrange("e p w -> p e w").bitcast(I32)
+            )
+            return tile
+
+        def load_gate(first, last, name):
+            tile = held([P, 2, (last - first) * C], F32, name)
+            nc.sync.dma_start(
+                tile[:], gate[0 : 2 * P, first * C : last * C].rearrange("(t p) j -> p t j", p=P)
+            )
+            return tile
+
+        ident = held([P, P], F32, "ident")
+        make_identity(nc, ident[:])
+
+        by_row = "e s q w -> q (e s) w"
+        x_plane = load_scales(nc.sync, x_scales.rearrange("o q w -> q o w"), "x_plane")
+        x_table = held([P, T], U32, "x_table")
+        nc.sync.dma_start(x_table[:].bitcast(I32), x_words[0].rearrange("p t r -> p (t r)").bitcast(I32))
+        w3_plane = load_scales(nc.gpsimd, w3_scales.rearrange(by_row), "w3_plane")
+        w2_plane = load_scales(nc.gpsimd, w2_scales.rearrange(by_row), "w2_plane")
+
+        w1, w3, w2, gates = {}, {}, {}, {}
+        w1[0] = load_words(w1_words, 0, 2, "w1_0")
+        w3[0] = load_words(w3_words, 0, 2, "w3_0")
+        w1_plane = load_scales(nc.sync, w1_scales.rearrange(by_row), "w1_plane")
+        w1[1] = load_words(w1_words, 2, 4, "w1_1")
+        w3[1] = load_words(w3_words, 2, 4, "w3_1")
+        w2[0] = load_words(w2_words, 0, 2, "w2_0")
+        gates[0] = load_gate(0, 2, "gate_0")
+        w1[2] = load_words(w1_words, 4, 8, "w1_2")
+        w3[2] = load_words(w3_words, 4, 8, "w3_2")
+        w2[1] = load_words(w2_words, 2, 4, "w2_1")
+        gates[1] = load_gate(2, 4, "gate_1")
+        w2[2] = load_words(w2_words, 4, 8, "w2_2")
+        gates[2] = load_gate(4, 8, "gate_2")
+        gate_last = held([P, S], F32, "gate_last")
+        nc.sync.dma_start(gate_last[:], gate[2 * P : 3 * P, :])
+
+        zero = held([P, 1], F32, "zero")
+        nc.vector.memset(zero[:], 0.0)
+        warm = held([P, 1], F32, "warm")
+        nc.scalar.activation(warm[:], zero[:], SILU)
+
+        xs = held([P, S], U8, "xs")
+        nc.vector.tensor_copy(xs[:], x_plane[:].indirect(offsets[:]))
+        xg = {}
+        for first, last in WORD_GATHERS:
+            tile = held([P, (last - first) * C], U32, f"xg_{first}")
+            nc.vector.tensor_copy(tile[:], x_table[:].indirect(slots(first, last)))
+            for e in range(first, last):
+                xg[e] = tile[:, (e - first) * C : (e - first + 1) * C]
+
+        gated = [held([P, 2, (last - first) * C], F32, f"gated_{first}") for first, last in GROUPS]
+        gated_last = held([P, S], F32, "gated_last")
+
+        y_last = None
+        for pair in range(E // 2):
+            g = min(pair, 2)
+            first = GROUPS[g][0]
+            ht_ps = psum.tile([P, 2, 2, C], F32, name="ht_ps", bufs=2)
+            for x in range(2):
+                e = 2 * pair + x
+                a_ps = psum.tile([P, H], F32, name="a_ps", bufs=2)
+                b_ps = psum.tile([P, H], F32, name="b_ps", bufs=2)
+                for acc, words, plane in ((a_ps, w1[g], w1_plane), (b_ps, w3[g], w3_plane)):
+                    nc.tensor.matmul_mx(
+                        acc[:],
+                        lhsT=xg[e].bitcast(FP8X4),
+                        lhsT_scale=xs[:, e * C : (e + 1) * C],
+                        rhs=words[:, e - first, :].bitcast(FP4X4),
+                        rhs_scale=plane[:, e * H : (e + 1) * H],
+                        start=True,
+                        stop=True,
+                    )
+                act = ring.tile([P, 2, P, 2], F32, name="act")
+                nc.scalar.activation(act[:], a_ps[:].rearrange("s (q u v) -> s u q v", u=2, v=2), SILU)
+                h = ring.tile([P, 2, P, 2], BF16, name="h")
+                nc.vector.tensor_tensor(h[:], b_ps[:].rearrange("s (q u v) -> s u q v", u=2, v=2), act[:], MULT)
+                h_words = h[:].rearrange("s u q v -> s (u q v)").bitcast(F32)
+                for u in range(2):
+                    nc.tensor.transpose(ht_ps[:, x, u, :], h_words[:, u * P : (u + 1) * P], ident[:])
+            ht = ring.tile([P, 2 * C * 4], BF16, name="ht", align_bytes=64)
+            nc.scalar.copy(
+                ht[:].bitcast(F32).rearrange("q (x s u) -> q x s u", x=2, u=2),
+                ht_ps[:].rearrange("q x u s -> q x s u"),
+            )
+            h_codes = ring.tile([P, 2 * C], U32, name="h_codes", align_bytes=64)
+            h_plane = ring.tile([P, 2 * C], U8, name="h_plane", align_bytes=64)
+            nc.vector.quantize_mx(out=h_codes[:].bitcast(FP8X4), scales=h_plane[:], in_=ht[:])
+
+            y_ps = psum.tile([P, 2, 2 * C], F32, name="y_ps")
+            if pair % 2 == 0:
+                y_last = psum.tile([P, 4 * C], F32, name="y_last")
+            for t in range(3):
+                for x in range(2):
+                    e = 2 * pair + x
+                    if t < 2:
+                        acc = y_ps[:, t, x * C : (x + 1) * C]
+                    else:
+                        acc = y_last[:, (e % 4) * C : (e % 4 + 1) * C]
+                    nc.tensor.matmul_mx(
+                        acc,
+                        lhsT=w2[g][:, e - first, 2 * t * P : 2 * (t + 1) * P].bitcast(FP4X4),
+                        lhsT_scale=w2_plane[:, e * N + t * P : e * N + (t + 1) * P],
+                        rhs=h_codes[:, x * C : (x + 1) * C].bitcast(FP8X4),
+                        rhs_scale=h_plane[:, x * C : (x + 1) * C],
+                        start=True,
+                        stop=True,
+                    )
+            cols = slice((2 * pair - first) * C, (2 * pair - first + 2) * C)
+            nc.vector.tensor_tensor(gated[g][:, :, cols], y_ps[:], gates[g][:, :, cols], MULT)
+            if pair % 2 == 1:
+                cols = slice((pair - 1) * 2 * C, (pair + 1) * 2 * C)
+                nc.vector.tensor_tensor(gated_last[:, cols], y_last[:], gate_last[:, cols], MULT)
+
+        windows = [keep.tile([P, T], F32, name=f"window_{t}") for t in range(3)]
+        for t in range(3):
+            for half in range(2):
+                nc.scalar.copy(
+                    windows[t][:, half * T // 2 : (half + 1) * T // 2], zero[:].to_broadcast([P, T // 2])
+                )
+        for g, (first, last) in enumerate(GROUPS):
+            for t in range(2):
+                nc.vector.tensor_copy(windows[t][:].indirect(slots(first, last)), gated[g][:, t, :])
+        for t in range(2):
+            nc.sync.dma_start(out[t * P : (t + 1) * P, :], windows[t][:])
+        nc.vector.tensor_copy(windows[2][:].indirect(offsets[:]), gated_last[:])
+        nc.sync.dma_start(out[2 * P : 3 * P, :], windows[2][:])

@@ -20,7 +20,6 @@ MULT = mybir.AluOpType.mult
 SILU = mybir.ActivationFunctionType.Silu
 
 GROUPS = ((0, 2), (2, 4), (4, 8))
-WORD_GATHERS = ((0, 2), (2, 8))
 
 
 def tile_moe_pkd_glu_silu_kernel(
@@ -45,7 +44,8 @@ def tile_moe_pkd_glu_silu_kernel(
             experts, width = scales.shape[1], scales.shape[2]
             plane = held([P, experts * width], U8, name)
             words = plane[:].bitcast(I32)
-            nc.vector.memset(words, 0)
+            if name == "x_plane":
+                nc.vector.memset(words, 0)
             rows = scales.rearrange("(q r) e w -> r q e w", r=4)
             for r in range(4):
                 queue.dma_start(
@@ -53,13 +53,20 @@ def tile_moe_pkd_glu_silu_kernel(
                 )
             return plane
 
-        def load_words(words, first, last, name):
+        def load_planes(queue, scales, first, last, planes, name):
+            width = scales.shape[3]
+            plane = load_scales(queue, scales[first:last].rearrange("e s q w -> q (e s) w"), name)
+            for e in range(first, last):
+                planes[e] = plane[:, (e - first) * width : (e - first + 1) * width]
+
+        def load_words(words, first, last, into, name):
             width = words.shape[3]
             tile = held([P, last - first, width], U8, name)
             nc.sync.dma_start(
                 tile[:].bitcast(I32), words[first:last, 0].rearrange("e p w -> p e w").bitcast(I32)
             )
-            return tile
+            for e in range(first, last):
+                into[e] = tile[:, e - first, :]
 
         def load_gate(first, last, name):
             tile = held([P, 2, (last - first) * C], F32, name)
@@ -71,26 +78,27 @@ def tile_moe_pkd_glu_silu_kernel(
         ident = held([P, P], F32, "ident")
         make_identity(nc, ident[:])
 
-        by_row = "e s q w -> q (e s) w"
+        w1, w3, w2, gates = {}, {}, {}, {}
+        w1_plane, w3_plane, w2_plane = {}, {}, {}
         x_plane = load_scales(nc.sync, x_scales.rearrange("o q w -> q o w"), "x_plane")
         x_table = held([P, T], U32, "x_table")
         nc.sync.dma_start(x_table[:].bitcast(I32), x_words[0].rearrange("p t r -> p (t r)").bitcast(I32))
-        w3_plane = load_scales(nc.gpsimd, w3_scales.rearrange(by_row), "w3_plane")
-        w2_plane = load_scales(nc.gpsimd, w2_scales.rearrange(by_row), "w2_plane")
-
-        w1, w3, w2, gates = {}, {}, {}, {}
-        w1[0] = load_words(w1_words, 0, 2, "w1_0")
-        w3[0] = load_words(w3_words, 0, 2, "w3_0")
-        w1_plane = load_scales(nc.sync, w1_scales.rearrange(by_row), "w1_plane")
-        w1[1] = load_words(w1_words, 2, 4, "w1_1")
-        w3[1] = load_words(w3_words, 2, 4, "w3_1")
-        w2[0] = load_words(w2_words, 0, 2, "w2_0")
+        load_planes(nc.sync, w1_scales, 0, 8, w1_plane, "w1_plane_0")
+        load_planes(nc.sync, w3_scales, 0, 8, w3_plane, "w3_plane_0")
+        load_words(w1_words, 0, 2, w1, "w1_0")
+        load_words(w3_words, 0, 2, w3, "w3_0")
+        load_words(w1_words, 2, 4, w1, "w1_2")
+        load_words(w3_words, 2, 4, w3, "w3_2")
+        load_words(w1_words, 4, 6, w1, "w1_4")
+        load_words(w3_words, 4, 6, w3, "w3_4")
+        load_words(w1_words, 6, 8, w1, "w1_6")
+        load_words(w3_words, 6, 8, w3, "w3_6")
+        load_planes(nc.sync, w2_scales, 0, 8, w2_plane, "w2_plane_0")
+        load_words(w2_words, 0, 2, w2, "w2_0")
         gates[0] = load_gate(0, 2, "gate_0")
-        w1[2] = load_words(w1_words, 4, 8, "w1_2")
-        w3[2] = load_words(w3_words, 4, 8, "w3_2")
-        w2[1] = load_words(w2_words, 2, 4, "w2_1")
+        load_words(w2_words, 2, 4, w2, "w2_2")
         gates[1] = load_gate(2, 4, "gate_1")
-        w2[2] = load_words(w2_words, 4, 8, "w2_2")
+        load_words(w2_words, 4, 8, w2, "w2_4")
         gates[2] = load_gate(4, 8, "gate_2")
         gate_last = held([P, S], F32, "gate_last")
         nc.sync.dma_start(gate_last[:], gate[2 * P : 3 * P, :])
@@ -100,34 +108,50 @@ def tile_moe_pkd_glu_silu_kernel(
         warm = held([P, 1], F32, "warm")
         nc.scalar.activation(warm[:], zero[:], SILU)
 
-        xs = held([P, S], U8, "xs")
-        nc.vector.tensor_copy(xs[:], x_plane[:].indirect(offsets[:]))
-        xg = {}
-        for first, last in WORD_GATHERS:
-            tile = held([P, (last - first) * C], U32, f"xg_{first}")
-            nc.vector.tensor_copy(tile[:], x_table[:].indirect(slots(first, last)))
+        xg, xs = {}, {}
+
+        def gather(first, last):
+            words = held([P, (last - first) * C], U32, f"xg_{first}")
+            nc.vector.tensor_copy(words[:], x_table[:].indirect(slots(first, last)))
+            plane = held([P, (last - first) * C], U8, f"xs_{first}")
+            nc.vector.tensor_copy(plane[:], x_plane[:].indirect(slots(first, last)))
             for e in range(first, last):
-                xg[e] = tile[:, (e - first) * C : (e - first + 1) * C]
+                xg[e] = words[:, (e - first) * C : (e - first + 1) * C]
+                xs[e] = plane[:, (e - first) * C : (e - first + 1) * C]
 
         gated = [held([P, 2, (last - first) * C], F32, f"gated_{first}") for first, last in GROUPS]
         gated_last = held([P, S], F32, "gated_last")
 
-        y_last = None
+        hq = {}
+
+        def down(acc, e, t):
+            nc.tensor.matmul_mx(
+                acc,
+                lhsT=w2[e][:, 2 * t * P : 2 * (t + 1) * P].bitcast(FP4X4),
+                lhsT_scale=w2_plane[e][:, t * P : (t + 1) * P],
+                rhs=hq[e][0].bitcast(FP8X4),
+                rhs_scale=hq[e][1],
+                start=True,
+                stop=True,
+            )
+
         for pair in range(E // 2):
             g = min(pair, 2)
             first = GROUPS[g][0]
+            if 2 * pair == first:
+                gather(*GROUPS[g])
             ht_ps = psum.tile([P, 2, 2, C], F32, name="ht_ps", bufs=2)
             for x in range(2):
                 e = 2 * pair + x
                 a_ps = psum.tile([P, H], F32, name="a_ps", bufs=2)
                 b_ps = psum.tile([P, H], F32, name="b_ps", bufs=2)
-                for acc, words, plane in ((a_ps, w1[g], w1_plane), (b_ps, w3[g], w3_plane)):
+                for acc, words, plane in ((a_ps, w1, w1_plane), (b_ps, w3, w3_plane)):
                     nc.tensor.matmul_mx(
                         acc[:],
                         lhsT=xg[e].bitcast(FP8X4),
-                        lhsT_scale=xs[:, e * C : (e + 1) * C],
-                        rhs=words[:, e - first, :].bitcast(FP4X4),
-                        rhs_scale=plane[:, e * H : (e + 1) * H],
+                        lhsT_scale=xs[e],
+                        rhs=words[e].bitcast(FP4X4),
+                        rhs_scale=plane[e],
                         start=True,
                         stop=True,
                     )
@@ -143,34 +167,24 @@ def tile_moe_pkd_glu_silu_kernel(
                 ht[:].bitcast(F32).rearrange("q (x s u) -> q x s u", x=2, u=2),
                 ht_ps[:].rearrange("q x u s -> q x s u"),
             )
-            h_codes = ring.tile([P, 2 * C], U32, name="h_codes", align_bytes=64)
-            h_plane = ring.tile([P, 2 * C], U8, name="h_plane", align_bytes=64)
+            h_codes = held([P, 2 * C], U32, f"h_codes_{pair}")
+            h_plane = held([P, 2 * C], U8, f"h_plane_{pair}")
             nc.vector.quantize_mx(out=h_codes[:].bitcast(FP8X4), scales=h_plane[:], in_=ht[:])
 
+            for x in range(2):
+                hq[2 * pair + x] = (h_codes[:, x * C : (x + 1) * C], h_plane[:, x * C : (x + 1) * C])
             y_ps = psum.tile([P, 2, 2 * C], F32, name="y_ps")
-            if pair % 2 == 0:
-                y_last = psum.tile([P, 4 * C], F32, name="y_last")
-            for t in range(3):
+            for t in range(2):
                 for x in range(2):
-                    e = 2 * pair + x
-                    if t < 2:
-                        acc = y_ps[:, t, x * C : (x + 1) * C]
-                    else:
-                        acc = y_last[:, (e % 4) * C : (e % 4 + 1) * C]
-                    nc.tensor.matmul_mx(
-                        acc,
-                        lhsT=w2[g][:, e - first, 2 * t * P : 2 * (t + 1) * P].bitcast(FP4X4),
-                        lhsT_scale=w2_plane[:, e * N + t * P : e * N + (t + 1) * P],
-                        rhs=h_codes[:, x * C : (x + 1) * C].bitcast(FP8X4),
-                        rhs_scale=h_plane[:, x * C : (x + 1) * C],
-                        start=True,
-                        stop=True,
-                    )
+                    down(y_ps[:, t, x * C : (x + 1) * C], 2 * pair + x, t)
             cols = slice((2 * pair - first) * C, (2 * pair - first + 2) * C)
-            nc.vector.tensor_tensor(gated[g][:, :, cols], y_ps[:], gates[g][:, :, cols], MULT)
-            if pair % 2 == 1:
-                cols = slice((pair - 1) * 2 * C, (pair + 1) * 2 * C)
-                nc.vector.tensor_tensor(gated_last[:, cols], y_last[:], gate_last[:, cols], MULT)
+            nc.scalar.copy(gated[g][:, :, cols], y_ps[:])
+
+        for half in range(2):
+            y_last = psum.tile([P, 4 * C], F32, name="y_last")
+            for x in range(4):
+                down(y_last[:, x * C : (x + 1) * C], 4 * half + x, 2)
+            nc.scalar.copy(gated_last[:, half * 4 * C : (half + 1) * 4 * C], y_last[:])
 
         windows = [keep.tile([P, T], F32, name=f"window_{t}") for t in range(3)]
         for t in range(3):
@@ -180,8 +194,10 @@ def tile_moe_pkd_glu_silu_kernel(
                 )
         for g, (first, last) in enumerate(GROUPS):
             for t in range(2):
-                nc.vector.tensor_copy(windows[t][:].indirect(slots(first, last)), gated[g][:, t, :])
+                nc.vector.tensor_tensor(
+                    windows[t][:].indirect(slots(first, last)), gated[g][:, t, :], gates[g][:, t, :], MULT
+                )
         for t in range(2):
             nc.sync.dma_start(out[t * P : (t + 1) * P, :], windows[t][:])
-        nc.vector.tensor_copy(windows[2][:].indirect(offsets[:]), gated_last[:])
+        nc.vector.tensor_tensor(windows[2][:].indirect(offsets[:]), gated_last[:], gate_last[:], MULT)
         nc.sync.dma_start(out[2 * P : 3 * P, :], windows[2][:])

@@ -19,7 +19,7 @@ FP4X4 = mybir.dt.float4_e2m1fn_x4
 MULT = mybir.AluOpType.mult
 SILU = mybir.ActivationFunctionType.Silu
 
-GROUPS = ((0, 2), (2, 4), (4, 8))
+GATHERS = {0: 2, 2: 4, 4: 8}
 
 
 def tile_moe_pkd_glu_silu_kernel(
@@ -28,8 +28,8 @@ def tile_moe_pkd_glu_silu_kernel(
     nc = tc.nc
     with ExitStack() as ctx:
         keep = ctx.enter_context(tc.tile_pool(name="keep", bufs=1))
-        ring = ctx.enter_context(tc.tile_pool(name="ring", bufs=3))
-        psum = ctx.enter_context(tc.psum_pool(name="psum", bufs=1))
+        ring = ctx.enter_context(tc.tile_pool(name="ring", bufs=4))
+        psum = ctx.enter_context(tc.psum_pool(name="psum", bufs=2))
 
         def held(shape, dtype, name):
             return keep.tile(shape, dtype, name=name, align_bytes=64)
@@ -40,89 +40,94 @@ def tile_moe_pkd_glu_silu_kernel(
         def slots(first, last):
             return offsets[:, first * C // 16 : last * C // 16]
 
-        def load_scales(queue, scales, name):
-            experts, width = scales.shape[1], scales.shape[2]
-            plane = held([P, experts * width], U8, name)
+        def load_scale_rows(plane, scales, rows):
+            by_row = scales.rearrange("(q r) e w -> r q e w", r=4)
             words = plane[:].bitcast(I32)
-            if name == "x_plane":
-                nc.vector.memset(words, 0)
-            rows = scales.rearrange("(q r) e w -> r q e w", r=4)
-            for r in range(4):
-                queue.dma_start(
-                    words[r:P:32, :].rearrange("q (e w) -> q e w", e=experts), rows[r].bitcast(I32)
+            for r in rows:
+                nc.sync.dma_start(
+                    words[r:P:32, :].rearrange("q (e w) -> q e w", e=scales.shape[1]), by_row[r].bitcast(I32)
                 )
-            return plane
 
-        def load_planes(queue, scales, first, last, planes, name):
+        def expert_rows(scales, first, last):
+            return scales[first:last].rearrange("e s q w -> q (e s) w")
+
+        def new_plane(scales, first, last, planes, name):
             width = scales.shape[3]
-            plane = load_scales(queue, scales[first:last].rearrange("e s q w -> q (e s) w"), name)
+            plane = held([P, (last - first) * width], U8, f"{name}_{first}")
             for e in range(first, last):
                 planes[e] = plane[:, (e - first) * width : (e - first + 1) * width]
+            return plane
+
+        def load_plane(scales, first, last, planes, name):
+            load_scale_rows(new_plane(scales, first, last, planes, name), expert_rows(scales, first, last), range(4))
 
         def load_words(words, first, last, into, name):
-            width = words.shape[3]
-            tile = held([P, last - first, width], U8, name)
+            tile = held([P, last - first, words.shape[3]], U8, f"{name}_{first}")
             nc.sync.dma_start(
                 tile[:].bitcast(I32), words[first:last, 0].rearrange("e p w -> p e w").bitcast(I32)
             )
             for e in range(first, last):
                 into[e] = tile[:, e - first, :]
 
-        def load_gate(first, last, name):
-            tile = held([P, 2, (last - first) * C], F32, name)
-            nc.sync.dma_start(
-                tile[:], gate[0 : 2 * P, first * C : last * C].rearrange("(t p) j -> p t j", p=P)
-            )
+        def load_gate(t, first, last):
+            tile = held([P, (last - first) * C], F32, f"gate_{t}_{first}")
+            nc.sync.dma_start(tile[:], gate[t * P : (t + 1) * P, first * C : last * C])
+            for e in range(first, last, 2):
+                gates[t, e // 2] = tile[:, (e - first) * C : (e - first + 2) * C]
             return tile
-
-        ident = held([P, P], F32, "ident")
-        make_identity(nc, ident[:])
 
         w1, w3, w2, gates = {}, {}, {}, {}
         w1_plane, w3_plane, w2_plane = {}, {}, {}
-        x_plane = load_scales(nc.sync, x_scales.rearrange("o q w -> q o w"), "x_plane")
+
+        x_plane = held([P, T], U8, "x_plane")
+        nc.vector.memset(x_plane[:].bitcast(I32), 0)
+        load_scale_rows(x_plane, x_scales.rearrange("o q w -> q o w"), range(4))
+        first_plane = new_plane(w1_scales, 0, 4, w1_plane, "w1_plane")
+        load_scale_rows(first_plane, expert_rows(w1_scales, 0, 4), range(1))
         x_table = held([P, T], U32, "x_table")
         nc.sync.dma_start(x_table[:].bitcast(I32), x_words[0].rearrange("p t r -> p (t r)").bitcast(I32))
-        load_planes(nc.sync, w1_scales, 0, 8, w1_plane, "w1_plane_0")
-        load_planes(nc.sync, w3_scales, 0, 8, w3_plane, "w3_plane_0")
-        load_words(w1_words, 0, 2, w1, "w1_0")
-        load_words(w3_words, 0, 2, w3, "w3_0")
-        load_words(w1_words, 2, 4, w1, "w1_2")
-        load_words(w3_words, 2, 4, w3, "w3_2")
-        load_words(w1_words, 4, 6, w1, "w1_4")
-        load_words(w3_words, 4, 6, w3, "w3_4")
-        load_words(w1_words, 6, 8, w1, "w1_6")
-        load_words(w3_words, 6, 8, w3, "w3_6")
-        load_planes(nc.sync, w2_scales, 0, 8, w2_plane, "w2_plane_0")
-        load_words(w2_words, 0, 2, w2, "w2_0")
-        gates[0] = load_gate(0, 2, "gate_0")
-        load_words(w2_words, 2, 4, w2, "w2_2")
-        gates[1] = load_gate(2, 4, "gate_1")
-        load_words(w2_words, 4, 8, w2, "w2_4")
-        gates[2] = load_gate(4, 8, "gate_2")
-        gate_last = held([P, S], F32, "gate_last")
-        nc.sync.dma_start(gate_last[:], gate[2 * P : 3 * P, :])
+        load_words(w1_words, 0, 2, w1, "w1")
+        load_words(w3_words, 0, 2, w3, "w3")
+        load_scale_rows(first_plane, expert_rows(w1_scales, 0, 4), range(1, 4))
+        load_plane(w3_scales, 0, 4, w3_plane, "w3_plane")
+        load_words(w1_words, 2, 4, w1, "w1")
+        load_words(w3_words, 2, 4, w3, "w3")
+        load_plane(w2_scales, 0, 8, w2_plane, "w2_plane")
+        load_words(w2_words, 0, 2, w2, "w2")
+        load_gate(0, 0, 2)
+        load_plane(w1_scales, 4, 8, w1_plane, "w1_plane")
+        load_plane(w3_scales, 4, 8, w3_plane, "w3_plane")
+        load_words(w1_words, 4, 6, w1, "w1")
+        load_words(w3_words, 4, 6, w3, "w3")
+        load_words(w1_words, 6, 8, w1, "w1")
+        load_gate(1, 0, 2)
+        load_words(w3_words, 6, 8, w3, "w3")
+        load_words(w2_words, 2, 4, w2, "w2")
+        load_gate(0, 2, 4)
+        load_words(w2_words, 4, 8, w2, "w2")
+        gate_last = load_gate(2, 0, E)
+        load_gate(1, 2, 8)
+        load_gate(0, 4, 8)
+
+        ident = held([P, P], F32, "ident")
+        make_identity(nc, ident[:])
 
         zero = held([P, 1], F32, "zero")
         nc.vector.memset(zero[:], 0.0)
         warm = held([P, 1], F32, "warm")
         nc.scalar.activation(warm[:], zero[:], SILU)
 
-        xg, xs = {}, {}
+        xg, xs, hq, y = {}, {}, {}, {}
+        y_last = held([P, S], F32, "y_last")
 
         def gather(first, last):
-            words = held([P, (last - first) * C], U32, f"xg_{first}")
-            nc.vector.tensor_copy(words[:], x_table[:].indirect(slots(first, last)))
             plane = held([P, (last - first) * C], U8, f"xs_{first}")
             nc.vector.tensor_copy(plane[:], x_plane[:].indirect(slots(first, last)))
+            words = held([P, (last - first) * C], U32, f"xg_{first}")
+            nc.vector.tensor_copy(words[:], x_table[:].indirect(slots(first, last)))
             for e in range(first, last):
                 xg[e] = words[:, (e - first) * C : (e - first + 1) * C]
                 xs[e] = plane[:, (e - first) * C : (e - first + 1) * C]
-
-        gated = [held([P, 2, (last - first) * C], F32, f"gated_{first}") for first, last in GROUPS]
-        gated_last = held([P, S], F32, "gated_last")
-
-        hq = {}
 
         def down(acc, e, t):
             nc.tensor.matmul_mx(
@@ -135,16 +140,28 @@ def tile_moe_pkd_glu_silu_kernel(
                 stop=True,
             )
 
+        def down_pair(pair, banks):
+            y_ps = psum.tile([P, 2, 2 * C], F32, name=f"y_ps_{pair}", tag=banks)
+            for t in range(2):
+                for x in range(2):
+                    down(y_ps[:, t, x * C : (x + 1) * C], 2 * pair + x, t)
+            y[pair] = held([P, 2, 2 * C], F32, f"y_{pair}")
+            nc.scalar.copy(y[pair][:], y_ps[:])
+
+        def down_last(half, banks):
+            y_ps = psum.tile([P, 4 * C], F32, name=f"y_last_ps_{half}", tag=banks)
+            for x in range(4):
+                down(y_ps[:, x * C : (x + 1) * C], 4 * half + x, 2)
+            nc.scalar.copy(y_last[:, half * 4 * C : (half + 1) * 4 * C], y_ps[:])
+
         for pair in range(E // 2):
-            g = min(pair, 2)
-            first = GROUPS[g][0]
-            if 2 * pair == first:
-                gather(*GROUPS[g])
-            ht_ps = psum.tile([P, 2, 2, C], F32, name="ht_ps", bufs=2)
+            if 2 * pair in GATHERS:
+                gather(2 * pair, GATHERS[2 * pair])
+            ht_ps = psum.tile([P, 2, 2, C], F32, name="ht_ps", tag="ht")
             for x in range(2):
                 e = 2 * pair + x
-                a_ps = psum.tile([P, H], F32, name="a_ps", bufs=2)
-                b_ps = psum.tile([P, H], F32, name="b_ps", bufs=2)
+                a_ps = psum.tile([P, H], F32, name="a_ps")
+                b_ps = psum.tile([P, H], F32, name="b_ps")
                 for acc, words, plane in ((a_ps, w1, w1_plane), (b_ps, w3, w3_plane)):
                     nc.tensor.matmul_mx(
                         acc[:],
@@ -170,34 +187,28 @@ def tile_moe_pkd_glu_silu_kernel(
             h_codes = held([P, 2 * C], U32, f"h_codes_{pair}")
             h_plane = held([P, 2 * C], U8, f"h_plane_{pair}")
             nc.vector.quantize_mx(out=h_codes[:].bitcast(FP8X4), scales=h_plane[:], in_=ht[:])
-
             for x in range(2):
                 hq[2 * pair + x] = (h_codes[:, x * C : (x + 1) * C], h_plane[:, x * C : (x + 1) * C])
-            y_ps = psum.tile([P, 2, 2 * C], F32, name="y_ps")
-            for t in range(2):
-                for x in range(2):
-                    down(y_ps[:, t, x * C : (x + 1) * C], 2 * pair + x, t)
-            cols = slice((2 * pair - first) * C, (2 * pair - first + 2) * C)
-            nc.scalar.copy(gated[g][:, :, cols], y_ps[:])
 
-        for half in range(2):
-            y_last = psum.tile([P, 4 * C], F32, name="y_last")
-            for x in range(4):
-                down(y_last[:, x * C : (x + 1) * C], 4 * half + x, 2)
-            nc.scalar.copy(gated_last[:, half * 4 * C : (half + 1) * 4 * C], y_last[:])
+            if pair < 2:
+                down_pair(pair, "y")
+
+        down_last(0, "ht")
+        down_pair(2, "ht")
+        down_pair(3, "y")
+        down_last(1, "y")
 
         windows = [keep.tile([P, T], F32, name=f"window_{t}") for t in range(3)]
-        for t in range(3):
+        nc.vector.memset(windows[0][:], 0.0)
+        for window in windows[1:]:
             for half in range(2):
-                nc.scalar.copy(
-                    windows[t][:, half * T // 2 : (half + 1) * T // 2], zero[:].to_broadcast([P, T // 2])
-                )
-        for g, (first, last) in enumerate(GROUPS):
+                nc.scalar.copy(window[:, half * T // 2 : (half + 1) * T // 2], zero[:].to_broadcast([P, T // 2]))
+        for pair in range(E // 2):
             for t in range(2):
                 nc.vector.tensor_tensor(
-                    windows[t][:].indirect(slots(first, last)), gated[g][:, t, :], gates[g][:, t, :], MULT
+                    windows[t][:].indirect(slots(2 * pair, 2 * pair + 2)), y[pair][:, t, :], gates[t, pair], MULT
                 )
         for t in range(2):
             nc.sync.dma_start(out[t * P : (t + 1) * P, :], windows[t][:])
-        nc.vector.tensor_tensor(windows[2][:].indirect(offsets[:]), gated_last[:], gate_last[:], MULT)
+        nc.vector.tensor_tensor(windows[2][:].indirect(offsets[:]), y_last[:], gate_last[:], MULT)
         nc.sync.dma_start(out[2 * P : 3 * P, :], windows[2][:])

@@ -19,7 +19,8 @@ FP4X4 = mybir.dt.float4_e2m1fn_x4
 MULT = mybir.AluOpType.mult
 SILU = mybir.ActivationFunctionType.Silu
 
-GATHERS = {0: 2, 2: 4, 4: 8}
+GATHERS = {0: 2, 2: 8}
+UNITS = ((0, 1), (1, 2), (2, 4), (4, 6), (6, 8))
 
 
 def tile_moe_pkd_glu_silu_kernel(
@@ -82,31 +83,29 @@ def tile_moe_pkd_glu_silu_kernel(
         x_plane = held([P, T], U8, "x_plane")
         nc.vector.memset(x_plane[:].bitcast(I32), 0)
         load_scale_rows(x_plane, x_scales.rearrange("o q w -> q o w"), range(4))
-        first_plane = new_plane(w1_scales, 0, 4, w1_plane, "w1_plane")
-        load_scale_rows(first_plane, expert_rows(w1_scales, 0, 4), range(1))
+        load_words(w1_words, 0, 2, w1, "w1")
         x_table = held([P, T], U32, "x_table")
         nc.sync.dma_start(x_table[:].bitcast(I32), x_words[0].rearrange("p t r -> p (t r)").bitcast(I32))
-        load_words(w1_words, 0, 2, w1, "w1")
+        load_plane(w1_scales, 0, 4, w1_plane, "w1_plane")
         load_words(w3_words, 0, 2, w3, "w3")
-        load_scale_rows(first_plane, expert_rows(w1_scales, 0, 4), range(1, 4))
         load_plane(w3_scales, 0, 4, w3_plane, "w3_plane")
         load_words(w1_words, 2, 4, w1, "w1")
-        load_words(w3_words, 2, 4, w3, "w3")
         load_plane(w2_scales, 0, 8, w2_plane, "w2_plane")
+        load_words(w3_words, 2, 4, w3, "w3")
         load_words(w2_words, 0, 2, w2, "w2")
         load_gate(0, 0, 2)
         load_plane(w1_scales, 4, 8, w1_plane, "w1_plane")
-        load_plane(w3_scales, 4, 8, w3_plane, "w3_plane")
         load_words(w1_words, 4, 6, w1, "w1")
         load_words(w3_words, 4, 6, w3, "w3")
+        load_plane(w3_scales, 4, 8, w3_plane, "w3_plane")
         load_words(w1_words, 6, 8, w1, "w1")
         load_gate(1, 0, 2)
+        load_gate(0, 2, 4)
         load_words(w3_words, 6, 8, w3, "w3")
         load_words(w2_words, 2, 4, w2, "w2")
-        load_gate(0, 2, 4)
-        load_words(w2_words, 4, 8, w2, "w2")
         gate_last = load_gate(2, 0, E)
         load_gate(1, 2, 8)
+        load_words(w2_words, 4, 8, w2, "w2")
         load_gate(0, 4, 8)
 
         ident = held([P, P], F32, "ident")
@@ -140,13 +139,16 @@ def tile_moe_pkd_glu_silu_kernel(
                 stop=True,
             )
 
-        def down_pair(pair, banks):
-            y_ps = psum.tile([P, 2, 2 * C], F32, name=f"y_ps_{pair}", tag=banks)
-            for t in range(2):
+        def down_pair(pair, row_tiles, banks):
+            name = f"y_{pair}_{row_tiles[0]}"
+            y_ps = psum.tile([P, len(row_tiles), 2 * C], F32, name=name + "_ps", tag=banks)
+            for i, t in enumerate(row_tiles):
                 for x in range(2):
-                    down(y_ps[:, t, x * C : (x + 1) * C], 2 * pair + x, t)
-            y[pair] = held([P, 2, 2 * C], F32, f"y_{pair}")
-            nc.scalar.copy(y[pair][:], y_ps[:])
+                    down(y_ps[:, i, x * C : (x + 1) * C], 2 * pair + x, t)
+            y_sb = held([P, len(row_tiles), 2 * C], F32, name)
+            nc.scalar.copy(y_sb[:], y_ps[:])
+            for i, t in enumerate(row_tiles):
+                y[t, pair] = y_sb[:, i, :]
 
         def down_last(half, banks):
             y_ps = psum.tile([P, 4 * C], F32, name=f"y_last_ps_{half}", tag=banks)
@@ -154,12 +156,13 @@ def tile_moe_pkd_glu_silu_kernel(
                 down(y_ps[:, x * C : (x + 1) * C], 4 * half + x, 2)
             nc.scalar.copy(y_last[:, half * 4 * C : (half + 1) * 4 * C], y_ps[:])
 
-        for pair in range(E // 2):
-            if 2 * pair in GATHERS:
-                gather(2 * pair, GATHERS[2 * pair])
-            ht_ps = psum.tile([P, 2, 2, C], F32, name="ht_ps", tag="ht")
-            for x in range(2):
-                e = 2 * pair + x
+        for first, last in UNITS:
+            if first in GATHERS:
+                gather(first, GATHERS[first])
+            count = last - first
+            ht_ps = psum.tile([P, count, 2, C], F32, name="ht_ps", tag="ht")
+            for e in range(first, last):
+                x = e - first
                 a_ps = psum.tile([P, H], F32, name="a_ps")
                 b_ps = psum.tile([P, H], F32, name="b_ps")
                 for acc, words, plane in ((a_ps, w1, w1_plane), (b_ps, w3, w3_plane)):
@@ -179,24 +182,25 @@ def tile_moe_pkd_glu_silu_kernel(
                 h_words = h[:].rearrange("s u q v -> s (u q v)").bitcast(F32)
                 for u in range(2):
                     nc.tensor.transpose(ht_ps[:, x, u, :], h_words[:, u * P : (u + 1) * P], ident[:])
-            ht = ring.tile([P, 2 * C * 4], BF16, name="ht", align_bytes=64)
+            ht = ring.tile([P, count * C * 4], BF16, name="ht", align_bytes=64)
             nc.scalar.copy(
-                ht[:].bitcast(F32).rearrange("q (x s u) -> q x s u", x=2, u=2),
+                ht[:].bitcast(F32).rearrange("q (x s u) -> q x s u", x=count, u=2),
                 ht_ps[:].rearrange("q x u s -> q x s u"),
             )
-            h_codes = held([P, 2 * C], U32, f"h_codes_{pair}")
-            h_plane = held([P, 2 * C], U8, f"h_plane_{pair}")
+            h_codes = held([P, count * C], U32, f"h_codes_{first}")
+            h_plane = held([P, count * C], U8, f"h_plane_{first}")
             nc.vector.quantize_mx(out=h_codes[:].bitcast(FP8X4), scales=h_plane[:], in_=ht[:])
-            for x in range(2):
-                hq[2 * pair + x] = (h_codes[:, x * C : (x + 1) * C], h_plane[:, x * C : (x + 1) * C])
+            for x in range(count):
+                hq[first + x] = (h_codes[:, x * C : (x + 1) * C], h_plane[:, x * C : (x + 1) * C])
 
-            if pair < 2:
-                down_pair(pair, "y")
+            if last == 2:
+                down_pair(0, (0,), "y")
+                down_pair(0, (1,), "y")
+            if last > 2:
+                down_pair(first // 2, (0, 1), "y")
 
-        down_last(0, "ht")
-        down_pair(2, "ht")
-        down_pair(3, "y")
-        down_last(1, "y")
+        for half in range(2):
+            down_last(half, "y")
 
         windows = [keep.tile([P, T], F32, name=f"window_{t}") for t in range(3)]
         nc.vector.memset(windows[0][:], 0.0)
@@ -206,7 +210,7 @@ def tile_moe_pkd_glu_silu_kernel(
         for pair in range(E // 2):
             for t in range(2):
                 nc.vector.tensor_tensor(
-                    windows[t][:].indirect(slots(2 * pair, 2 * pair + 2)), y[pair][:, t, :], gates[t, pair], MULT
+                    windows[t][:].indirect(slots(2 * pair, 2 * pair + 2)), y[t, pair], gates[t, pair], MULT
                 )
         for t in range(2):
             nc.sync.dma_start(out[t * P : (t + 1) * P, :], windows[t][:])

@@ -113,8 +113,6 @@ def tile_moe_pkd_glu_silu_kernel(
 
         zero = held([P, 1], F32, "zero")
         nc.vector.memset(zero[:], 0.0)
-        warm = held([P, 1], F32, "warm")
-        nc.scalar.activation(warm[:], zero[:], SILU)
 
         xg, xs, hq, y = {}, {}, {}, {}
         y_last = held([P, S], F32, "y_last")

@@ -19,8 +19,9 @@ FP4X4 = mybir.dt.float4_e2m1fn_x4
 MULT = mybir.AluOpType.mult
 SILU = mybir.ActivationFunctionType.Silu
 
-GATHERS = {0: 2, 2: 8}
-UNITS = ((0, 1), (1, 2), (2, 4), (4, 6), (6, 8))
+A_BANK = ("a0", "a1", "e", "c", "e", "b0", "a0", "a1")
+B_BANK = ("b0", "b1", "f", "b1", "b0", "b1", "f", "b1")
+H_SLOT = ("h0", "h1", "h0", "h1", "h0", "h1", "h0", "h1")
 
 
 def tile_moe_pkd_glu_silu_kernel(
@@ -30,22 +31,21 @@ def tile_moe_pkd_glu_silu_kernel(
     with ExitStack() as ctx:
         keep = ctx.enter_context(tc.tile_pool(name="keep", bufs=1))
         ring = ctx.enter_context(tc.tile_pool(name="ring", bufs=4))
-        psum = ctx.enter_context(tc.psum_pool(name="psum", bufs=2))
+        psum = ctx.enter_context(tc.psum_pool(name="psum", bufs=1))
 
         def held(shape, dtype, name):
             return keep.tile(shape, dtype, name=name, align_bytes=64)
 
         offsets = keep.tile([P, S // 16], U16, name="offsets")
-        nc.sync.dma_start(offsets[:], offs)
 
         def slots(first, last):
             return offsets[:, first * C // 16 : last * C // 16]
 
-        def load_scale_rows(plane, scales, rows):
+        def load_scale_rows(plane, scales, rows, queue):
             by_row = scales.rearrange("(q r) e w -> r q e w", r=4)
             words = plane[:].bitcast(I32)
             for r in rows:
-                nc.sync.dma_start(
+                queue.dma_start(
                     words[r:P:32, :].rearrange("q (e w) -> q e w", e=scales.shape[1]), by_row[r].bitcast(I32)
                 )
 
@@ -60,7 +60,8 @@ def tile_moe_pkd_glu_silu_kernel(
             return plane
 
         def load_plane(scales, first, last, planes, name):
-            load_scale_rows(new_plane(scales, first, last, planes, name), expert_rows(scales, first, last), range(4))
+            plane = new_plane(scales, first, last, planes, name)
+            load_scale_rows(plane, expert_rows(scales, first, last), range(4), nc.sync)
 
         def load_words(words, first, last, into, name):
             tile = held([P, last - first, words.shape[3]], U8, f"{name}_{first}")
@@ -70,43 +71,40 @@ def tile_moe_pkd_glu_silu_kernel(
             for e in range(first, last):
                 into[e] = tile[:, e - first, :]
 
-        def load_gate(t, first, last):
-            tile = held([P, (last - first) * C], F32, f"gate_{t}_{first}")
-            nc.sync.dma_start(tile[:], gate[t * P : (t + 1) * P, first * C : last * C])
-            for e in range(first, last, 2):
-                gates[t, e // 2] = tile[:, (e - first) * C : (e - first + 2) * C]
-            return tile
+        gates = held([P, S], F32, "gates")
 
-        w1, w3, w2, gates = {}, {}, {}, {}
+        def load_gate(first, last):
+            nc.sync.dma_start(gates[:, first * C : last * C], gate[:P, first * C : last * C])
+
+        w1, w3, w2 = {}, {}, {}
         w1_plane, w3_plane, w2_plane = {}, {}, {}
 
-        x_plane = held([P, T], U8, "x_plane")
-        nc.vector.memset(x_plane[:].bitcast(I32), 0)
-        load_scale_rows(x_plane, x_scales.rearrange("o q w -> q o w"), range(4))
-        load_words(w1_words, 0, 2, w1, "w1")
         x_table = held([P, T], U32, "x_table")
         nc.sync.dma_start(x_table[:].bitcast(I32), x_words[0].rearrange("p t r -> p (t r)").bitcast(I32))
+        nc.sync.dma_start(offsets[:], offs)
+        x_plane = held([P, T], U8, "x_plane")
+        nc.vector.memset(x_plane[:].bitcast(I32), 0)
+        load_scale_rows(x_plane, x_scales.rearrange("o q w -> q o w"), range(4), nc.sync)
+        load_words(w1_words, 0, 2, w1, "w1")
         load_plane(w1_scales, 0, 4, w1_plane, "w1_plane")
         load_words(w3_words, 0, 2, w3, "w3")
         load_plane(w3_scales, 0, 4, w3_plane, "w3_plane")
         load_words(w1_words, 2, 4, w1, "w1")
-        load_plane(w2_scales, 0, 8, w2_plane, "w2_plane")
         load_words(w3_words, 2, 4, w3, "w3")
+        load_plane(w2_scales, 0, 4, w2_plane, "w2_plane")
         load_words(w2_words, 0, 2, w2, "w2")
-        load_gate(0, 0, 2)
+        load_gate(0, 2)
         load_plane(w1_scales, 4, 8, w1_plane, "w1_plane")
+        load_plane(w3_scales, 4, 8, w3_plane, "w3_plane")
         load_words(w1_words, 4, 6, w1, "w1")
         load_words(w3_words, 4, 6, w3, "w3")
-        load_plane(w3_scales, 4, 8, w3_plane, "w3_plane")
-        load_words(w1_words, 6, 8, w1, "w1")
-        load_gate(1, 0, 2)
-        load_gate(0, 2, 4)
-        load_words(w3_words, 6, 8, w3, "w3")
         load_words(w2_words, 2, 4, w2, "w2")
-        gate_last = load_gate(2, 0, E)
-        load_gate(1, 2, 8)
+        load_gate(2, 4)
+        load_words(w1_words, 6, 8, w1, "w1")
+        load_words(w3_words, 6, 8, w3, "w3")
+        load_plane(w2_scales, 4, 8, w2_plane, "w2_plane")
         load_words(w2_words, 4, 8, w2, "w2")
-        load_gate(0, 4, 8)
+        load_gate(4, E)
 
         ident = held([P, P], F32, "ident")
         make_identity(nc, ident[:])
@@ -115,16 +113,18 @@ def tile_moe_pkd_glu_silu_kernel(
         nc.vector.memset(zero[:], 0.0)
 
         xg, xs, hq, y = {}, {}, {}, {}
-        y_last = held([P, S], F32, "y_last")
 
-        def gather(first, last):
+        def gather_plane(first, last):
             plane = held([P, (last - first) * C], U8, f"xs_{first}")
             nc.vector.tensor_copy(plane[:], x_plane[:].indirect(slots(first, last)))
-            words = held([P, (last - first) * C], U32, f"xg_{first}")
+            for e in range(first, last):
+                xs[e] = plane[:, (e - first) * C : (e - first + 1) * C]
+
+        def gather_words(first, last, tag):
+            words = keep.tile([P, (last - first) * C], U32, name=f"xg_{first}", tag=tag, align_bytes=64)
             nc.vector.tensor_copy(words[:], x_table[:].indirect(slots(first, last)))
             for e in range(first, last):
                 xg[e] = words[:, (e - first) * C : (e - first + 1) * C]
-                xs[e] = plane[:, (e - first) * C : (e - first + 1) * C]
 
         def down(acc, e, t):
             nc.tensor.matmul_mx(
@@ -137,80 +137,121 @@ def tile_moe_pkd_glu_silu_kernel(
                 stop=True,
             )
 
-        def down_pair(pair, row_tiles, banks):
-            name = f"y_{pair}_{row_tiles[0]}"
-            y_ps = psum.tile([P, len(row_tiles), 2 * C], F32, name=name + "_ps", tag=banks)
+        def down_tile(pair, t, bank, pool, tag):
+            y_ps = psum.tile([P, 2 * C], F32, name=f"y_ps_{pair}_{t}", tag=bank)
+            for x in range(2):
+                down(y_ps[:, x * C : (x + 1) * C], 2 * pair + x, t)
+            y[t, pair] = pool.tile([P, 2 * C], F32, name=f"y_{pair}_{t}", tag=tag, align_bytes=64)
+            nc.scalar.copy(y[t, pair][:], y_ps[:])
+
+        def down_gated(pair, row_tiles, bank, tag):
+            count = len(row_tiles)
+            y_ps = psum.tile([P, count, 2 * C], F32, name=f"y_ps_{pair}_{row_tiles[0]}", tag=bank)
             for i, t in enumerate(row_tiles):
                 for x in range(2):
                     down(y_ps[:, i, x * C : (x + 1) * C], 2 * pair + x, t)
-            y_sb = held([P, len(row_tiles), 2 * C], F32, name)
-            nc.scalar.copy(y_sb[:], y_ps[:])
+            gated = keep.tile([P, count, 2 * C], F32, name=f"gated_{pair}", tag=tag, align_bytes=64)
+            weight = gates[:, 2 * pair * C : (2 * pair + 2) * C].unsqueeze(1).to_broadcast([P, count, 2 * C])
+            nc.vector.tensor_tensor(gated[:], y_ps[:], weight, MULT)
             for i, t in enumerate(row_tiles):
-                y[t, pair] = y_sb[:, i, :]
+                y[t, pair] = gated[:, i, :]
 
-        def down_last(half, banks):
-            y_ps = psum.tile([P, 4 * C], F32, name=f"y_last_ps_{half}", tag=banks)
+        def down_half(t, bank):
+            y_ps = psum.tile([P, 4 * C], F32, name=f"y_half_ps_{t}", tag=bank)
             for x in range(4):
-                down(y_ps[:, x * C : (x + 1) * C], 4 * half + x, 2)
-            nc.scalar.copy(y_last[:, half * 4 * C : (half + 1) * 4 * C], y_ps[:])
+                down(y_ps[:, x * C : (x + 1) * C], 4 + x, t)
+            y[t, 2] = held([P, 4 * C], F32, f"y_half_{t}")
+            nc.scalar.copy(y[t, 2][:], y_ps[:])
 
-        for first, last in UNITS:
-            if first in GATHERS:
-                gather(first, GATHERS[first])
+        def up(e):
+            a_ps = psum.tile([P, H], F32, name=f"a_ps_{e}", tag=A_BANK[e])
+            b_ps = psum.tile([P, H], F32, name=f"b_ps_{e}", tag=B_BANK[e])
+            for acc, words, plane in ((a_ps, w1, w1_plane), (b_ps, w3, w3_plane)):
+                nc.tensor.matmul_mx(
+                    acc[:],
+                    lhsT=xg[e].bitcast(FP8X4),
+                    lhsT_scale=xs[e],
+                    rhs=words[e].bitcast(FP4X4),
+                    rhs_scale=plane[e],
+                    start=True,
+                    stop=True,
+                )
+            act = ring.tile([P, 2, P, 2], F32, name="act")
+            nc.scalar.activation(act[:], a_ps[:].rearrange("s (q u v) -> s u q v", u=2, v=2), SILU)
+            h[e] = keep.tile([P, 2, P, 2], BF16, name=f"h_{e}", tag=H_SLOT[e], align_bytes=64)
+            b_view = b_ps[:].rearrange("s (q u v) -> s u q v", u=2, v=2)
+            if e < 4:
+                nc.vector.tensor_tensor(h[e][:], b_view, act[:], MULT)
+            else:
+                lin = ring.tile([P, 2, P, 2], F32, name="lin")
+                nc.scalar.copy(lin[:], b_view)
+                nc.gpsimd.tensor_tensor(h[e][:], lin[:], act[:], MULT)
+
+        def turn(e, ht_ps, x):
+            h_words = h[e][:].rearrange("s u q v -> s (u q v)").bitcast(F32)
+            for u in range(2):
+                nc.tensor.transpose(ht_ps[:, x, u, :], h_words[:, u * P : (u + 1) * P], ident[:])
+
+        def quantise(first, last, ht):
             count = last - first
-            ht_ps = psum.tile([P, count, 2, C], F32, name="ht_ps", tag="ht")
-            for e in range(first, last):
-                x = e - first
-                a_ps = psum.tile([P, H], F32, name="a_ps")
-                b_ps = psum.tile([P, H], F32, name="b_ps")
-                for acc, words, plane in ((a_ps, w1, w1_plane), (b_ps, w3, w3_plane)):
-                    nc.tensor.matmul_mx(
-                        acc[:],
-                        lhsT=xg[e].bitcast(FP8X4),
-                        lhsT_scale=xs[e],
-                        rhs=words[e].bitcast(FP4X4),
-                        rhs_scale=plane[e],
-                        start=True,
-                        stop=True,
-                    )
-                act = ring.tile([P, 2, P, 2], F32, name="act")
-                nc.scalar.activation(act[:], a_ps[:].rearrange("s (q u v) -> s u q v", u=2, v=2), SILU)
-                h = ring.tile([P, 2, P, 2], BF16, name="h")
-                nc.vector.tensor_tensor(h[:], b_ps[:].rearrange("s (q u v) -> s u q v", u=2, v=2), act[:], MULT)
-                h_words = h[:].rearrange("s u q v -> s (u q v)").bitcast(F32)
-                for u in range(2):
-                    nc.tensor.transpose(ht_ps[:, x, u, :], h_words[:, u * P : (u + 1) * P], ident[:])
-            ht = ring.tile([P, count * C * 4], BF16, name="ht", align_bytes=64)
-            nc.scalar.copy(
-                ht[:].bitcast(F32).rearrange("q (x s u) -> q x s u", x=count, u=2),
-                ht_ps[:].rearrange("q x u s -> q x s u"),
-            )
             h_codes = held([P, count * C], U32, f"h_codes_{first}")
             h_plane = held([P, count * C], U8, f"h_plane_{first}")
-            nc.vector.quantize_mx(out=h_codes[:].bitcast(FP8X4), scales=h_plane[:], in_=ht[:])
+            nc.vector.quantize_mx(out=h_codes[:].bitcast(FP8X4), scales=h_plane[:], in_=ht)
             for x in range(count):
                 hq[first + x] = (h_codes[:, x * C : (x + 1) * C], h_plane[:, x * C : (x + 1) * C])
 
-            if last == 2:
-                down_pair(0, (0,), "y")
-                down_pair(0, (1,), "y")
-            if last > 2:
-                down_pair(first // 2, (0, 1), "y")
+        def hidden(first, last, bank, ht):
+            count = last - first
+            ht_ps = psum.tile([P, count, 2, C], F32, name=f"ht_ps_{first}", tag=bank)
+            for e in range(first, last):
+                up(e)
+                turn(e, ht_ps, e - first)
+            nc.scalar.copy(
+                ht.bitcast(F32).rearrange("q (x s u) -> q x s u", x=count, u=2),
+                ht_ps[:].rearrange("q x u s -> q x s u"),
+            )
 
-        for half in range(2):
-            down_last(half, "y")
+        def unit(first, last, bank, tag):
+            ht = keep.tile([P, (last - first) * C * 4], BF16, name=f"ht_{first}", tag=tag, align_bytes=64)
+            hidden(first, last, bank, ht[:])
+            quantise(first, last, ht[:])
+
+        h = {}
+        gather_words(0, 2, "xg_0")
+        gather_plane(0, 2)
+        gather_plane(2, E)
+        gather_words(2, 4, "x_plane")
+        unit(0, 1, "c", "ht_0")
+        unit(1, 2, "d", "h0")
+        gather_words(4, E, "xg_0")
+        down_tile(0, 0, "a0", keep, "y_0_0")
+        unit(2, 4, "a0", "ht_2")
+        down_gated(0, (1, 2), "a1", "ht_2")
+        ht_late = held([P, 4 * C * 4], BF16, "ht_late")
+        hidden(4, 6, "d", ht_late[:, : 2 * C * 4])
+        down_gated(1, (0,), "e", "gated_1")
+        down_tile(1, 1, "b0", keep, "y_1_1")
+        hidden(6, 8, "c", ht_late[:, 2 * C * 4 :])
+        quantise(4, E, ht_late[:])
+        down_tile(1, 2, "f", keep, "h1")
+        for t in range(3):
+            down_half(t, ("e", "b0", "d")[t])
 
         windows = [keep.tile([P, T], F32, name=f"window_{t}") for t in range(3)]
-        nc.vector.memset(windows[0][:], 0.0)
-        for window in windows[1:]:
-            for half in range(2):
-                nc.scalar.copy(window[:, half * T // 2 : (half + 1) * T // 2], zero[:].to_broadcast([P, T // 2]))
-        for pair in range(E // 2):
-            for t in range(2):
-                nc.vector.tensor_tensor(
-                    windows[t][:].indirect(slots(2 * pair, 2 * pair + 2)), y[t, pair], gates[t, pair], MULT
-                )
-        for t in range(2):
+        for window in windows[:2]:
+            nc.vector.memset(window[:], 0.0)
+        nc.scalar.copy(windows[2][:], zero[:].to_broadcast([P, T]))
+
+        def scatter(t, pair, first, last):
+            nc.vector.tensor_tensor(
+                windows[t][:].indirect(slots(first, last)), y[t, pair][:], gates[:, first * C : last * C], MULT
+            )
+
+        scatter(0, 0, 0, 2)
+        for t, pair in ((1, 0), (2, 0), (0, 1)):
+            nc.vector.tensor_copy(windows[t][:].indirect(slots(2 * pair, 2 * pair + 2)), y[t, pair])
+        scatter(1, 1, 2, 4)
+        scatter(2, 1, 2, 4)
+        for t in range(3):
+            scatter(t, 2, 4, E)
             nc.sync.dma_start(out[t * P : (t + 1) * P, :], windows[t][:])
-        nc.vector.tensor_tensor(windows[2][:].indirect(offsets[:]), y_last[:], gate_last[:], MULT)
-        nc.sync.dma_start(out[2 * P : 3 * P, :], windows[2][:])

@@ -19,9 +19,10 @@ FP4X4 = mybir.dt.float4_e2m1fn_x4
 MULT = mybir.AluOpType.mult
 SILU = mybir.ActivationFunctionType.Silu
 
-A_BANK = ("a0", "a1", "e", "c", "e", "b0", "a0", "a1")
-B_BANK = ("b0", "b1", "f", "b1", "b0", "b1", "f", "b1")
-H_SLOT = ("h0", "h1", "h0", "h1", "h0", "h1", "h0", "h1")
+A_BANK = ("a0", "a1", "e", "f", "e", "c", "a0", "f")
+B_BANK = ("b0", "b1", "b0", "b1", "c", "b1", "f", "b0")
+H_SLOT = ("h0", "h1", "h0", "h3", "h0", "h1", "h3", "h7")
+ACT_SLOT = ("act0", "act1", "act2", "h1", "act0", "act1", "act2", "act3")
 
 
 def tile_moe_pkd_glu_silu_kernel(
@@ -37,6 +38,7 @@ def tile_moe_pkd_glu_silu_kernel(
             return keep.tile(shape, dtype, name=name, align_bytes=64)
 
         offsets = keep.tile([P, S // 16], U16, name="offsets")
+        nc.sync.dma_start(offsets[:], offs)
 
         def slots(first, last):
             return offsets[:, first * C // 16 : last * C // 16]
@@ -79,13 +81,12 @@ def tile_moe_pkd_glu_silu_kernel(
         w1, w3, w2 = {}, {}, {}
         w1_plane, w3_plane, w2_plane = {}, {}, {}
 
-        x_table = held([P, T], U32, "x_table")
-        nc.sync.dma_start(x_table[:].bitcast(I32), x_words[0].rearrange("p t r -> p (t r)").bitcast(I32))
-        nc.sync.dma_start(offsets[:], offs)
         x_plane = held([P, T], U8, "x_plane")
         nc.vector.memset(x_plane[:].bitcast(I32), 0)
-        load_scale_rows(x_plane, x_scales.rearrange("o q w -> q o w"), range(4), nc.sync)
         load_words(w1_words, 0, 2, w1, "w1")
+        load_scale_rows(x_plane, x_scales.rearrange("o q w -> q o w"), range(4), nc.sync)
+        x_table = held([P, T], U32, "x_table")
+        nc.sync.dma_start(x_table[:].bitcast(I32), x_words[0].rearrange("p t r -> p (t r)").bitcast(I32))
         load_plane(w1_scales, 0, 4, w1_plane, "w1_plane")
         load_words(w3_words, 0, 2, w3, "w3")
         load_plane(w3_scales, 0, 4, w3_plane, "w3_plane")
@@ -144,6 +145,13 @@ def tile_moe_pkd_glu_silu_kernel(
             y[t, pair] = pool.tile([P, 2 * C], F32, name=f"y_{pair}_{t}", tag=tag, align_bytes=64)
             nc.scalar.copy(y[t, pair][:], y_ps[:])
 
+        def down_first():
+            y[0, 0] = held([P, 2 * C], F32, "y_0_0")
+            for e in range(2):
+                y_ps = psum.tile([P, C], F32, name=f"y_ps_first_{e}", tag=f"a{e}")
+                down(y_ps[:], e, 0)
+                nc.scalar.copy(y[0, 0][:, e * C : (e + 1) * C], y_ps[:])
+
         def down_gated(pair, row_tiles, bank, tag):
             count = len(row_tiles)
             y_ps = psum.tile([P, count, 2 * C], F32, name=f"y_ps_{pair}_{row_tiles[0]}", tag=bank)
@@ -176,7 +184,7 @@ def tile_moe_pkd_glu_silu_kernel(
                     start=True,
                     stop=True,
                 )
-            act = ring.tile([P, 2, P, 2], F32, name="act")
+            act = keep.tile([P, 2, P, 2], F32, name=f"act_{e}", tag=ACT_SLOT[e], align_bytes=64)
             nc.scalar.activation(act[:], a_ps[:].rearrange("s (q u v) -> s u q v", u=2, v=2), SILU)
             h[e] = keep.tile([P, 2, P, 2], BF16, name=f"h_{e}", tag=H_SLOT[e], align_bytes=64)
             b_view = b_ps[:].rearrange("s (q u v) -> s u q v", u=2, v=2)
@@ -204,7 +212,8 @@ def tile_moe_pkd_glu_silu_kernel(
             count = last - first
             ht_ps = psum.tile([P, count, 2, C], F32, name=f"ht_ps_{first}", tag=bank)
             for e in range(first, last):
-                up(e)
+                if e not in h:
+                    up(e)
                 turn(e, ht_ps, e - first)
             nc.scalar.copy(
                 ht.bitcast(F32).rearrange("q (x s u) -> q x s u", x=count, u=2),
@@ -217,30 +226,32 @@ def tile_moe_pkd_glu_silu_kernel(
             quantise(first, last, ht[:])
 
         h = {}
+        gather_plane(0, E)
         gather_words(0, 2, "xg_0")
-        gather_plane(0, 2)
-        gather_plane(2, E)
-        gather_words(2, 4, "x_plane")
+        gather_words(2, E, "xg_2")
         unit(0, 1, "c", "ht_0")
-        unit(1, 2, "d", "h0")
-        gather_words(4, E, "xg_0")
-        down_tile(0, 0, "a0", keep, "y_0_0")
-        unit(2, 4, "a0", "ht_2")
-        down_gated(0, (1, 2), "a1", "ht_2")
+        unit(1, 2, "d", "ht_1")
+        down_first()
+        unit(2, 4, "a1", "ht_2")
+        down_gated(0, (1, 2), "d", "ht_2")
         ht_late = held([P, 4 * C * 4], BF16, "ht_late")
-        hidden(4, 6, "d", ht_late[:, : 2 * C * 4])
-        down_gated(1, (0,), "e", "gated_1")
-        down_tile(1, 1, "b0", keep, "y_1_1")
-        hidden(6, 8, "c", ht_late[:, 2 * C * 4 :])
+        up(4)
+        up(5)
+        down_gated(1, (0, 1), "e", "gated_1")
+        up(6)
+        up(7)
+        hidden(4, 6, "f", ht_late[:, : 2 * C * 4])
+        hidden(6, 8, "d", ht_late[:, 2 * C * 4 :])
         quantise(4, E, ht_late[:])
-        down_tile(1, 2, "f", keep, "h1")
+        down_tile(1, 2, "b0", keep, "h7")
         for t in range(3):
-            down_half(t, ("e", "b0", "d")[t])
+            down_half(t, ("e", "f", "c")[t])
 
         windows = [keep.tile([P, T], F32, name=f"window_{t}") for t in range(3)]
-        for window in windows[:2]:
-            nc.vector.memset(window[:], 0.0)
-        nc.scalar.copy(windows[2][:], zero[:].to_broadcast([P, T]))
+        nc.vector.memset(windows[0][:], 0.0)
+        for window in windows[1:]:
+            for half in range(2):
+                nc.scalar.copy(window[:, half * T // 2 : (half + 1) * T // 2], zero[:].to_broadcast([P, T // 2]))
 
         def scatter(t, pair, first, last):
             nc.vector.tensor_tensor(
@@ -248,9 +259,8 @@ def tile_moe_pkd_glu_silu_kernel(
             )
 
         scatter(0, 0, 0, 2)
-        for t, pair in ((1, 0), (2, 0), (0, 1)):
+        for t, pair in ((1, 0), (2, 0), (0, 1), (1, 1)):
             nc.vector.tensor_copy(windows[t][:].indirect(slots(2 * pair, 2 * pair + 2)), y[t, pair])
-        scatter(1, 1, 2, 4)
         scatter(2, 1, 2, 4)
         for t in range(3):
             scatter(t, 2, 4, E)

@@ -19,6 +19,7 @@ FP4X4 = mybir.dt.float4_e2m1fn_x4
 MULT = mybir.AluOpType.mult
 SILU = mybir.ActivationFunctionType.Silu
 
+LATE = 64
 A_BANK = ("a0", "a1", "e", "f", "e", "c", "a0", "f")
 B_BANK = ("b0", "b1", "b0", "b1", "c", "b1", "f", "b0")
 H_SLOT = ("h0", "h1", "h0", "h3", "h0", "h1", "h3", "h7")
@@ -83,6 +84,9 @@ def tile_moe_pkd_glu_silu_kernel(
 
         x_plane = held([P, T], U8, "x_plane")
         nc.vector.memset(x_plane[:].bitcast(I32), 0)
+        zero = held([P, LATE], F32, "zero")
+        nc.vector.memset(zero[:], 0.0)
+        windows = [keep.tile([P, T], F32, name=f"window_{t}") for t in range(3)]
         load_words(w1_words, 0, 2, w1, "w1")
         load_scale_rows(x_plane, x_scales.rearrange("o q w -> q o w"), range(4), nc.sync)
         x_table = held([P, T], U32, "x_table")
@@ -96,7 +100,9 @@ def tile_moe_pkd_glu_silu_kernel(
         load_words(w2_words, 0, 2, w2, "w2")
         load_gate(0, 2)
         load_plane(w1_scales, 4, 8, w1_plane, "w1_plane")
+        nc.sync.dma_start(windows[1][:, T - LATE :], zero[:])
         load_plane(w3_scales, 4, 8, w3_plane, "w3_plane")
+        nc.sync.dma_start(windows[2][:, T - LATE :], zero[:])
         load_words(w1_words, 4, 6, w1, "w1")
         load_words(w3_words, 4, 6, w3, "w3")
         load_words(w2_words, 2, 4, w2, "w2")
@@ -109,9 +115,6 @@ def tile_moe_pkd_glu_silu_kernel(
 
         ident = held([P, P], F32, "ident")
         make_identity(nc, ident[:])
-
-        zero = held([P, 1], F32, "zero")
-        nc.vector.memset(zero[:], 0.0)
 
         xg, xs, hq, y = {}, {}, {}, {}
 
@@ -151,6 +154,19 @@ def tile_moe_pkd_glu_silu_kernel(
                 y_ps = psum.tile([P, C], F32, name=f"y_ps_first_{e}", tag=f"a{e}")
                 down(y_ps[:], e, 0)
                 nc.scalar.copy(y[0, 0][:, e * C : (e + 1) * C], y_ps[:])
+
+        def down_plain(pair, t, bank):
+            y_ps = psum.tile([P, 2 * C], F32, name=f"y_ps_side_{pair}", tag=bank)
+            for x in range(2):
+                down(y_ps[:, x * C : (x + 1) * C], 2 * pair + x, t)
+            plain = held([P, 2 * C], F32, f"y_side_{pair}")
+            nc.scalar.copy(plain[:], y_ps[:])
+            return plain
+
+        def gate_on_gpsimd(pair, t, plain, tag):
+            gated = keep.tile([P, 2 * C], F32, name=f"gated_side_{pair}", tag=tag, align_bytes=64)
+            nc.gpsimd.tensor_tensor(gated[:], plain[:], gates[:, 2 * pair * C : (2 * pair + 2) * C], MULT)
+            y[t, pair] = gated[:]
 
         def down_gated(pair, row_tiles, bank, tag):
             count = len(row_tiles)
@@ -225,6 +241,23 @@ def tile_moe_pkd_glu_silu_kernel(
             hidden(first, last, bank, ht[:])
             quantise(first, last, ht[:])
 
+        blank = held([P, H], BF16, "blank")
+        nc.vector.memset(blank[:].bitcast(I32), 0)
+        warm_codes = held([P, C], U32, "warm_codes")
+        warm_plane = held([P, H], U8, "warm_plane")
+        nc.vector.memset(warm_plane[:].bitcast(I32), 0)
+        nc.vector.quantize_mx(out=warm_codes[:].bitcast(FP8X4), scales=warm_plane[:, :C], in_=blank[:])
+        warm_ps = psum.tile([P, H], F32, name="warm_ps", tag="e")
+        for rep in range(5):
+            nc.tensor.matmul_mx(
+                warm_ps[:],
+                lhsT=warm_codes[:].bitcast(FP8X4),
+                lhsT_scale=warm_plane[:, :C],
+                rhs=w1[0].bitcast(FP4X4),
+                rhs_scale=warm_plane[:],
+                start=True,
+                stop=True,
+            )
         h = {}
         gather_plane(0, E)
         gather_words(0, 2, "xg_0")
@@ -232,26 +265,28 @@ def tile_moe_pkd_glu_silu_kernel(
         unit(0, 1, "c", "ht_0")
         unit(1, 2, "d", "ht_1")
         down_first()
+        down_gated(0, (1,), "d", "gated_0")
+        plain = down_plain(0, 2, "c")
         unit(2, 4, "a1", "ht_2")
-        down_gated(0, (1, 2), "d", "ht_2")
-        ht_late = held([P, 4 * C * 4], BF16, "ht_late")
+        gate_on_gpsimd(0, 2, plain, "ht_2")
         up(4)
+        down_gated(1, (0,), "e", "gated_1")
         up(5)
-        down_gated(1, (0, 1), "e", "gated_1")
+        gate_on_gpsimd(1, 1, down_plain(1, 1, "d"), "gated_side_1")
         up(6)
         up(7)
-        hidden(4, 6, "f", ht_late[:, : 2 * C * 4])
-        hidden(6, 8, "d", ht_late[:, 2 * C * 4 :])
-        quantise(4, E, ht_late[:])
-        down_tile(1, 2, "b0", keep, "h7")
-        for t in range(3):
-            down_half(t, ("e", "f", "c")[t])
+        unit(4, 6, "f", "ht_4")
+        down_tile(1, 2, "b0", keep, "h1")
+        unit(6, 8, "f", "ht_6")
+        down_tile(2, 0, "e", keep, "y_2_0")
+        down_tile(2, 1, "d", keep, "y_2_1")
+        down_tile(3, 0, "c", keep, "y_3_0")
+        down_tile(3, 1, "a0", keep, "y_3_1")
+        down_half(2, "b1")
 
-        windows = [keep.tile([P, T], F32, name=f"window_{t}") for t in range(3)]
         nc.vector.memset(windows[0][:], 0.0)
         for window in windows[1:]:
-            for half in range(2):
-                nc.scalar.copy(window[:, half * T // 2 : (half + 1) * T // 2], zero[:].to_broadcast([P, T // 2]))
+            nc.scalar.copy(window[:, : T - LATE], zero[:, :1].to_broadcast([P, T - LATE]))
 
         def scatter(t, pair, first, last):
             nc.vector.tensor_tensor(
@@ -262,6 +297,10 @@ def tile_moe_pkd_glu_silu_kernel(
         for t, pair in ((1, 0), (2, 0), (0, 1), (1, 1)):
             nc.vector.tensor_copy(windows[t][:].indirect(slots(2 * pair, 2 * pair + 2)), y[t, pair])
         scatter(2, 1, 2, 4)
-        for t in range(3):
-            scatter(t, 2, 4, E)
+        for pair in range(2, 4):
+            for t in range(2):
+                scatter(t, pair, 2 * pair, 2 * pair + 2)
+        for t in range(2):
             nc.sync.dma_start(out[t * P : (t + 1) * P, :], windows[t][:])
+        scatter(2, 2, 4, E)
+        nc.sync.dma_start(out[2 * P :, :], windows[2][:])

@@ -102,11 +102,11 @@ def tile_moe_pkd_glu_silu_kernel(
         load_plane(w1_scales, 4, 8, w1_plane, "w1_plane")
         nc.sync.dma_start(windows[1][:, T - LATE :], zero[:])
         load_plane(w3_scales, 4, 8, w3_plane, "w3_plane")
-        nc.sync.dma_start(windows[2][:, T - LATE :], zero[:])
         load_words(w1_words, 4, 6, w1, "w1")
         load_words(w3_words, 4, 6, w3, "w3")
         load_words(w2_words, 2, 4, w2, "w2")
         load_gate(2, 4)
+        nc.sync.dma_start(windows[2][:, T - LATE :], zero[:])
         load_words(w1_words, 6, 8, w1, "w1")
         load_words(w3_words, 6, 8, w3, "w3")
         load_plane(w2_scales, 4, 8, w2_plane, "w2_plane")
@@ -241,6 +241,8 @@ def tile_moe_pkd_glu_silu_kernel(
             hidden(first, last, bank, ht[:])
             quantise(first, last, ht[:])
 
+        h = {}
+        gather_plane(0, 2)
         blank = held([P, H], BF16, "blank")
         nc.vector.memset(blank[:].bitcast(I32), 0)
         warm_codes = held([P, C], U32, "warm_codes")
@@ -248,18 +250,17 @@ def tile_moe_pkd_glu_silu_kernel(
         nc.vector.memset(warm_plane[:].bitcast(I32), 0)
         nc.vector.quantize_mx(out=warm_codes[:].bitcast(FP8X4), scales=warm_plane[:, :C], in_=blank[:])
         warm_ps = psum.tile([P, H], F32, name="warm_ps", tag="e")
-        for rep in range(5):
+        for rep in range(4):
             nc.tensor.matmul_mx(
                 warm_ps[:],
                 lhsT=warm_codes[:].bitcast(FP8X4),
-                lhsT_scale=warm_plane[:, :C],
+                lhsT_scale=xs[0],
                 rhs=w1[0].bitcast(FP4X4),
                 rhs_scale=warm_plane[:],
                 start=True,
                 stop=True,
             )
-        h = {}
-        gather_plane(0, E)
+        gather_plane(2, E)
         gather_words(0, 2, "xg_0")
         gather_words(2, E, "xg_2")
         unit(0, 1, "c", "ht_0")
@@ -270,9 +271,8 @@ def tile_moe_pkd_glu_silu_kernel(
         unit(2, 4, "a1", "ht_2")
         gate_on_gpsimd(0, 2, plain, "ht_2")
         up(4)
-        down_gated(1, (0,), "e", "gated_1")
+        down_gated(1, (0, 1), "e", "gated_1")
         up(5)
-        gate_on_gpsimd(1, 1, down_plain(1, 1, "d"), "gated_side_1")
         up(6)
         up(7)
         unit(4, 6, "f", "ht_4")

@@ -19,11 +19,7 @@ FP4X4 = mybir.dt.float4_e2m1fn_x4
 MULT = mybir.AluOpType.mult
 SILU = mybir.ActivationFunctionType.Silu
 
-LATE = 64
-A_BANK = ("a0", "a1", "e", "f", "e", "c", "a0", "f")
-B_BANK = ("b0", "b1", "b0", "b1", "c", "b1", "f", "b0")
-H_SLOT = ("h0", "h1", "h0", "h3", "h0", "h1", "h3", "h7")
-ACT_SLOT = ("act0", "act1", "act2", "h1", "act0", "act1", "act2", "act3")
+DMA_CLEARED = 64
 
 
 def tile_moe_pkd_glu_silu_kernel(
@@ -32,11 +28,13 @@ def tile_moe_pkd_glu_silu_kernel(
     nc = tc.nc
     with ExitStack() as ctx:
         keep = ctx.enter_context(tc.tile_pool(name="keep", bufs=1))
-        ring = ctx.enter_context(tc.tile_pool(name="ring", bufs=4))
         psum = ctx.enter_context(tc.psum_pool(name="psum", bufs=1))
 
-        def held(shape, dtype, name):
-            return keep.tile(shape, dtype, name=name, align_bytes=64)
+        def held(shape, dtype, name, slot=None):
+            return keep.tile(shape, dtype, name=name, tag=slot or name, align_bytes=64)
+
+        def banked(shape, name, bank):
+            return psum.tile(shape, F32, name=name, tag=f"bank_{bank}")
 
         offsets = keep.tile([P, S // 16], U16, name="offsets")
         nc.sync.dma_start(offsets[:], offs)
@@ -44,33 +42,24 @@ def tile_moe_pkd_glu_silu_kernel(
         def slots(first, last):
             return offsets[:, first * C // 16 : last * C // 16]
 
-        def load_scale_rows(plane, scales, rows, queue):
+        def load_scale_rows(plane, scales):
             by_row = scales.rearrange("(q r) e w -> r q e w", r=4)
-            words = plane[:].bitcast(I32)
-            for r in rows:
-                queue.dma_start(
-                    words[r:P:32, :].rearrange("q (e w) -> q e w", e=scales.shape[1]), by_row[r].bitcast(I32)
+            as_int = plane[:].bitcast(I32)
+            for r in range(4):
+                nc.sync.dma_start(
+                    as_int[r:P:32, :].rearrange("q (e w) -> q e w", e=scales.shape[1]), by_row[r].bitcast(I32)
                 )
 
-        def expert_rows(scales, first, last):
-            return scales[first:last].rearrange("e s q w -> q (e s) w")
-
-        def new_plane(scales, first, last, planes, name):
+        def load_plane(scales, first, last, planes, name):
             width = scales.shape[3]
             plane = held([P, (last - first) * width], U8, f"{name}_{first}")
+            load_scale_rows(plane, scales[first:last].rearrange("e s q w -> q (e s) w"))
             for e in range(first, last):
                 planes[e] = plane[:, (e - first) * width : (e - first + 1) * width]
-            return plane
-
-        def load_plane(scales, first, last, planes, name):
-            plane = new_plane(scales, first, last, planes, name)
-            load_scale_rows(plane, expert_rows(scales, first, last), range(4), nc.sync)
 
         def load_words(words, first, last, into, name):
             tile = held([P, last - first, words.shape[3]], U8, f"{name}_{first}")
-            nc.sync.dma_start(
-                tile[:].bitcast(I32), words[first:last, 0].rearrange("e p w -> p e w").bitcast(I32)
-            )
+            nc.sync.dma_start(tile[:].bitcast(I32), words[first:last, 0].rearrange("e p w -> p e w").bitcast(I32))
             for e in range(first, last):
                 into[e] = tile[:, e - first, :]
 
@@ -79,16 +68,22 @@ def tile_moe_pkd_glu_silu_kernel(
         def load_gate(first, last):
             nc.sync.dma_start(gates[:, first * C : last * C], gate[:P, first * C : last * C])
 
-        w1, w3, w2 = {}, {}, {}
-        w1_plane, w3_plane, w2_plane = {}, {}, {}
+        def gate_of(first, last):
+            return gates[:, first * C : last * C]
 
         x_plane = held([P, T], U8, "x_plane")
         nc.vector.memset(x_plane[:].bitcast(I32), 0)
-        zero = held([P, LATE], F32, "zero")
+        zero = held([P, DMA_CLEARED], F32, "zero")
         nc.vector.memset(zero[:], 0.0)
-        windows = [keep.tile([P, T], F32, name=f"window_{t}") for t in range(3)]
+        windows = [keep.tile([P, T], F32, name=f"window_{t}") for t in range(N // P)]
+
+        def clear_tail(t):
+            nc.sync.dma_start(windows[t][:, T - DMA_CLEARED :], zero[:])
+
+        w1, w3, w2 = {}, {}, {}
+        w1_plane, w3_plane, w2_plane = {}, {}, {}
         load_words(w1_words, 0, 2, w1, "w1")
-        load_scale_rows(x_plane, x_scales.rearrange("o q w -> q o w"), range(4), nc.sync)
+        load_scale_rows(x_plane, x_scales.rearrange("o q w -> q o w"))
         x_table = held([P, T], U32, "x_table")
         nc.sync.dma_start(x_table[:].bitcast(I32), x_words[0].rearrange("p t r -> p (t r)").bitcast(I32))
         load_plane(w1_scales, 0, 4, w1_plane, "w1_plane")
@@ -99,36 +94,73 @@ def tile_moe_pkd_glu_silu_kernel(
         load_plane(w2_scales, 0, 4, w2_plane, "w2_plane")
         load_words(w2_words, 0, 2, w2, "w2")
         load_gate(0, 2)
-        load_plane(w1_scales, 4, 8, w1_plane, "w1_plane")
-        nc.sync.dma_start(windows[1][:, T - LATE :], zero[:])
-        load_plane(w3_scales, 4, 8, w3_plane, "w3_plane")
+        load_plane(w1_scales, 4, E, w1_plane, "w1_plane")
+        clear_tail(1)
+        load_plane(w3_scales, 4, E, w3_plane, "w3_plane")
         load_words(w1_words, 4, 6, w1, "w1")
         load_words(w3_words, 4, 6, w3, "w3")
         load_words(w2_words, 2, 4, w2, "w2")
         load_gate(2, 4)
-        nc.sync.dma_start(windows[2][:, T - LATE :], zero[:])
-        load_words(w1_words, 6, 8, w1, "w1")
-        load_words(w3_words, 6, 8, w3, "w3")
-        load_plane(w2_scales, 4, 8, w2_plane, "w2_plane")
-        load_words(w2_words, 4, 8, w2, "w2")
+        clear_tail(2)
+        load_words(w1_words, 6, E, w1, "w1")
+        load_words(w3_words, 6, E, w3, "w3")
+        load_plane(w2_scales, 4, E, w2_plane, "w2_plane")
+        load_words(w2_words, 4, E, w2, "w2")
         load_gate(4, E)
 
         ident = held([P, P], F32, "ident")
         make_identity(nc, ident[:])
 
-        xg, xs, hq, y = {}, {}, {}, {}
-
-        def gather_plane(first, last):
-            plane = held([P, (last - first) * C], U8, f"xs_{first}")
-            nc.vector.tensor_copy(plane[:], x_plane[:].indirect(slots(first, last)))
+        xg, h, hq = {}, {}, {}
+        xs = held([P, S], U8, "xs")
+        nc.vector.tensor_copy(xs[:], x_plane[:].indirect(offsets[:]))
+        for first, last in ((0, 2), (2, E)):
+            gathered = held([P, (last - first) * C], U32, f"xg_{first}")
+            nc.vector.tensor_copy(gathered[:], x_table[:].indirect(slots(first, last)))
             for e in range(first, last):
-                xs[e] = plane[:, (e - first) * C : (e - first + 1) * C]
+                xg[e] = gathered[:, (e - first) * C : (e - first + 1) * C]
 
-        def gather_words(first, last, tag):
-            words = keep.tile([P, (last - first) * C], U32, name=f"xg_{first}", tag=tag, align_bytes=64)
-            nc.vector.tensor_copy(words[:], x_table[:].indirect(slots(first, last)))
-            for e in range(first, last):
-                xg[e] = words[:, (e - first) * C : (e - first + 1) * C]
+        def up(e, a_bank, b_bank, act_slot, h_slot):
+            a_ps = banked([P, H], f"a_ps_{e}", a_bank)
+            b_ps = banked([P, H], f"b_ps_{e}", b_bank)
+            for acc, words, plane in ((a_ps, w1, w1_plane), (b_ps, w3, w3_plane)):
+                nc.tensor.matmul_mx(
+                    acc[:],
+                    lhsT=xg[e].bitcast(FP8X4),
+                    lhsT_scale=xs[:, e * C : (e + 1) * C],
+                    rhs=words[e].bitcast(FP4X4),
+                    rhs_scale=plane[e],
+                    start=True,
+                    stop=True,
+                )
+            act = held([P, 2, P, 2], F32, f"act_{e}", act_slot)
+            nc.scalar.activation(act[:], a_ps[:].rearrange("s (q u v) -> s u q v", u=2, v=2), SILU)
+            h[e] = held([P, 2, P, 2], BF16, f"h_{e}", h_slot)
+            b_view = b_ps[:].rearrange("s (q u v) -> s u q v", u=2, v=2)
+            if e < E // 2:
+                nc.vector.tensor_tensor(h[e][:], b_view, act[:], MULT)
+            else:
+                b_sb = held([P, 2, P, 2], F32, f"b_sb_{e}")
+                nc.scalar.copy(b_sb[:], b_view)
+                nc.gpsimd.tensor_tensor(h[e][:], b_sb[:], act[:], MULT)
+
+        def turn(e, ht_ps, x):
+            pairs = h[e][:].rearrange("s u q v -> s (u q v)").bitcast(F32)
+            for u in range(2):
+                nc.tensor.transpose(ht_ps[:, x, u, :], pairs[:, u * P : (u + 1) * P], ident[:])
+
+        def quantise(first, last, ht_ps):
+            count = last - first
+            ht = held([P, count * C * 4], BF16, f"ht_{first}")
+            nc.scalar.copy(
+                ht[:].bitcast(F32).rearrange("q (x s u) -> q x s u", x=count, u=2),
+                ht_ps[:].rearrange("q x u s -> q x s u"),
+            )
+            codes = held([P, count * C], U32, f"h_codes_{first}")
+            plane = held([P, count * C], U8, f"h_plane_{first}")
+            nc.vector.quantize_mx(out=codes[:].bitcast(FP8X4), scales=plane[:], in_=ht[:])
+            for x in range(count):
+                hq[first + x] = (codes[:, x * C : (x + 1) * C], plane[:, x * C : (x + 1) * C])
 
         def down(acc, e, t):
             nc.tensor.matmul_mx(
@@ -141,166 +173,90 @@ def tile_moe_pkd_glu_silu_kernel(
                 stop=True,
             )
 
-        def down_tile(pair, t, bank, pool, tag):
-            y_ps = psum.tile([P, 2 * C], F32, name=f"y_ps_{pair}_{t}", tag=bank)
-            for x in range(2):
-                down(y_ps[:, x * C : (x + 1) * C], 2 * pair + x, t)
-            y[t, pair] = pool.tile([P, 2 * C], F32, name=f"y_{pair}_{t}", tag=tag, align_bytes=64)
-            nc.scalar.copy(y[t, pair][:], y_ps[:])
-
-        def down_first():
-            y[0, 0] = held([P, 2 * C], F32, "y_0_0")
-            for e in range(2):
-                y_ps = psum.tile([P, C], F32, name=f"y_ps_first_{e}", tag=f"a{e}")
-                down(y_ps[:], e, 0)
-                nc.scalar.copy(y[0, 0][:, e * C : (e + 1) * C], y_ps[:])
-
-        def down_plain(pair, t, bank):
-            y_ps = psum.tile([P, 2 * C], F32, name=f"y_ps_side_{pair}", tag=bank)
-            for x in range(2):
-                down(y_ps[:, x * C : (x + 1) * C], 2 * pair + x, t)
-            plain = held([P, 2 * C], F32, f"y_side_{pair}")
-            nc.scalar.copy(plain[:], y_ps[:])
-            return plain
-
-        def gate_on_gpsimd(pair, t, plain, tag):
-            gated = keep.tile([P, 2 * C], F32, name=f"gated_side_{pair}", tag=tag, align_bytes=64)
-            nc.gpsimd.tensor_tensor(gated[:], plain[:], gates[:, 2 * pair * C : (2 * pair + 2) * C], MULT)
-            y[t, pair] = gated[:]
-
-        def down_gated(pair, row_tiles, bank, tag):
-            count = len(row_tiles)
-            y_ps = psum.tile([P, count, 2 * C], F32, name=f"y_ps_{pair}_{row_tiles[0]}", tag=bank)
-            for i, t in enumerate(row_tiles):
-                for x in range(2):
-                    down(y_ps[:, i, x * C : (x + 1) * C], 2 * pair + x, t)
-            gated = keep.tile([P, count, 2 * C], F32, name=f"gated_{pair}", tag=tag, align_bytes=64)
-            weight = gates[:, 2 * pair * C : (2 * pair + 2) * C].unsqueeze(1).to_broadcast([P, count, 2 * C])
-            nc.vector.tensor_tensor(gated[:], y_ps[:], weight, MULT)
-            for i, t in enumerate(row_tiles):
-                y[t, pair] = gated[:, i, :]
-
-        def down_half(t, bank):
-            y_ps = psum.tile([P, 4 * C], F32, name=f"y_half_ps_{t}", tag=bank)
-            for x in range(4):
-                down(y_ps[:, x * C : (x + 1) * C], 4 + x, t)
-            y[t, 2] = held([P, 4 * C], F32, f"y_half_{t}")
-            nc.scalar.copy(y[t, 2][:], y_ps[:])
-
-        def up(e):
-            a_ps = psum.tile([P, H], F32, name=f"a_ps_{e}", tag=A_BANK[e])
-            b_ps = psum.tile([P, H], F32, name=f"b_ps_{e}", tag=B_BANK[e])
-            for acc, words, plane in ((a_ps, w1, w1_plane), (b_ps, w3, w3_plane)):
-                nc.tensor.matmul_mx(
-                    acc[:],
-                    lhsT=xg[e].bitcast(FP8X4),
-                    lhsT_scale=xs[e],
-                    rhs=words[e].bitcast(FP4X4),
-                    rhs_scale=plane[e],
-                    start=True,
-                    stop=True,
-                )
-            act = keep.tile([P, 2, P, 2], F32, name=f"act_{e}", tag=ACT_SLOT[e], align_bytes=64)
-            nc.scalar.activation(act[:], a_ps[:].rearrange("s (q u v) -> s u q v", u=2, v=2), SILU)
-            h[e] = keep.tile([P, 2, P, 2], BF16, name=f"h_{e}", tag=H_SLOT[e], align_bytes=64)
-            b_view = b_ps[:].rearrange("s (q u v) -> s u q v", u=2, v=2)
-            if e < 4:
-                nc.vector.tensor_tensor(h[e][:], b_view, act[:], MULT)
-            else:
-                lin = ring.tile([P, 2, P, 2], F32, name="lin")
-                nc.scalar.copy(lin[:], b_view)
-                nc.gpsimd.tensor_tensor(h[e][:], lin[:], act[:], MULT)
-
-        def turn(e, ht_ps, x):
-            h_words = h[e][:].rearrange("s u q v -> s (u q v)").bitcast(F32)
-            for u in range(2):
-                nc.tensor.transpose(ht_ps[:, x, u, :], h_words[:, u * P : (u + 1) * P], ident[:])
-
-        def quantise(first, last, ht):
-            count = last - first
-            h_codes = held([P, count * C], U32, f"h_codes_{first}")
-            h_plane = held([P, count * C], U8, f"h_plane_{first}")
-            nc.vector.quantize_mx(out=h_codes[:].bitcast(FP8X4), scales=h_plane[:], in_=ht)
-            for x in range(count):
-                hq[first + x] = (h_codes[:, x * C : (x + 1) * C], h_plane[:, x * C : (x + 1) * C])
-
-        def hidden(first, last, bank, ht):
-            count = last - first
-            ht_ps = psum.tile([P, count, 2, C], F32, name=f"ht_ps_{first}", tag=bank)
+        def down_plain(t, first, last, bank, slot=None):
+            y_ps = banked([P, (last - first) * C], f"y_ps_{t}_{first}", bank)
             for e in range(first, last):
-                if e not in h:
-                    up(e)
-                turn(e, ht_ps, e - first)
-            nc.scalar.copy(
-                ht.bitcast(F32).rearrange("q (x s u) -> q x s u", x=count, u=2),
-                ht_ps[:].rearrange("q x u s -> q x s u"),
-            )
+                down(y_ps[:, (e - first) * C : (e - first + 1) * C], e, t)
+            y_sb = held([P, (last - first) * C], F32, f"y_{t}_{first}", slot)
+            nc.scalar.copy(y_sb[:], y_ps[:])
+            return y_sb[:]
 
-        def unit(first, last, bank, tag):
-            ht = keep.tile([P, (last - first) * C * 4], BF16, name=f"ht_{first}", tag=tag, align_bytes=64)
-            hidden(first, last, bank, ht[:])
-            quantise(first, last, ht[:])
+        def down_gated(row_tiles, first, last, bank):
+            shape = [P, len(row_tiles), (last - first) * C]
+            y_ps = banked(shape, f"y_ps_{row_tiles[0]}_{first}", bank)
+            for i, t in enumerate(row_tiles):
+                for e in range(first, last):
+                    down(y_ps[:, i, (e - first) * C : (e - first + 1) * C], e, t)
+            gated = held(shape, F32, f"gated_{first}")
+            nc.vector.tensor_tensor(gated[:], y_ps[:], gate_of(first, last).unsqueeze(1).to_broadcast(shape), MULT)
+            return gated
 
-        h = {}
-        gather_plane(0, 2)
-        blank = held([P, H], BF16, "blank")
-        nc.vector.memset(blank[:].bitcast(I32), 0)
-        warm_codes = held([P, C], U32, "warm_codes")
-        warm_plane = held([P, H], U8, "warm_plane")
-        nc.vector.memset(warm_plane[:].bitcast(I32), 0)
-        nc.vector.quantize_mx(out=warm_codes[:].bitcast(FP8X4), scales=warm_plane[:, :C], in_=blank[:])
-        warm_ps = psum.tile([P, H], F32, name="warm_ps", tag="e")
-        for rep in range(4):
-            nc.tensor.matmul_mx(
-                warm_ps[:],
-                lhsT=warm_codes[:].bitcast(FP8X4),
-                lhsT_scale=xs[0],
-                rhs=w1[0].bitcast(FP4X4),
-                rhs_scale=warm_plane[:],
-                start=True,
-                stop=True,
-            )
-        gather_plane(2, E)
-        gather_words(0, 2, "xg_0")
-        gather_words(2, E, "xg_2")
-        unit(0, 1, "c", "ht_0")
-        unit(1, 2, "d", "ht_1")
-        down_first()
-        down_gated(0, (1,), "d", "gated_0")
-        plain = down_plain(0, 2, "c")
-        unit(2, 4, "a1", "ht_2")
-        gate_on_gpsimd(0, 2, plain, "ht_2")
-        up(4)
-        down_gated(1, (0, 1), "e", "gated_1")
-        up(5)
-        up(6)
-        up(7)
-        unit(4, 6, "f", "ht_4")
-        down_tile(1, 2, "b0", keep, "h1")
-        unit(6, 8, "f", "ht_6")
-        down_tile(2, 0, "e", keep, "y_2_0")
-        down_tile(2, 1, "d", keep, "y_2_1")
-        down_tile(3, 0, "c", keep, "y_3_0")
-        down_tile(3, 1, "a0", keep, "y_3_1")
-        down_half(2, "b1")
+        for e in range(2):
+            ht_ps = banked([P, 1, 2, C], f"ht_ps_{e}", 4 + e)
+            up(e, a_bank=e, b_bank=2 + e, act_slot=f"act_{e}", h_slot=f"h_{e}")
+            turn(e, ht_ps, 0)
+            quantise(e, e + 1, ht_ps)
+        y_0_0 = held([P, 2 * C], F32, "y_0_0")
+        for e in range(2):
+            y_ps = banked([P, C], f"y_ps_first_{e}", e)
+            down(y_ps[:], e, 0)
+            nc.scalar.copy(y_0_0[:, e * C : (e + 1) * C], y_ps[:])
+        gated_0 = down_gated((1,), 0, 2, bank=5)
+        y_2_0 = down_plain(2, 0, 2, bank=4)
+
+        ht_ps = banked([P, 2, 2, C], "ht_ps_2", 1)
+        up(2, a_bank=6, b_bank=2, act_slot="act_2", h_slot="h_0")
+        turn(2, ht_ps, 0)
+        up(3, a_bank=7, b_bank=3, act_slot="h_1", h_slot="h_3")
+        turn(3, ht_ps, 1)
+        quantise(2, 4, ht_ps)
+
+        gated_2_0 = held([P, 2 * C], F32, "gated_2_0", "ht_2")
+        nc.gpsimd.tensor_tensor(gated_2_0[:], y_2_0, gate_of(0, 2), MULT)
+
+        up(4, a_bank=6, b_bank=4, act_slot="act_0", h_slot="h_0")
+        gated_2 = down_gated((0, 1), 2, 4, bank=6)
+        up(5, a_bank=4, b_bank=3, act_slot="act_1", h_slot="h_1")
+        up(6, a_bank=0, b_bank=7, act_slot="act_2", h_slot="h_3")
+        up(7, a_bank=7, b_bank=2, act_slot="act_7", h_slot="h_7")
+
+        ht_ps = banked([P, 2, 2, C], "ht_ps_4", 7)
+        for x in range(2):
+            turn(4 + x, ht_ps, x)
+        quantise(4, 6, ht_ps)
+        y_2_2 = down_plain(2, 2, 4, bank=2, slot="h_1")
+        ht_ps = banked([P, 2, 2, C], "ht_ps_6", 7)
+        for x in range(2):
+            turn(6 + x, ht_ps, x)
+        quantise(6, E, ht_ps)
+
+        y_0_4 = down_plain(0, 4, 6, bank=6)
+        y_1_4 = down_plain(1, 4, 6, bank=5)
+        y_0_6 = down_plain(0, 6, E, bank=4)
+        y_1_6 = down_plain(1, 6, E, bank=0)
+        y_2_4 = down_plain(2, 4, E, bank=3)
 
         nc.vector.memset(windows[0][:], 0.0)
         for window in windows[1:]:
-            nc.scalar.copy(window[:, : T - LATE], zero[:, :1].to_broadcast([P, T - LATE]))
+            nc.scalar.copy(window[:, : T - DMA_CLEARED], zero[:, :1].to_broadcast([P, T - DMA_CLEARED]))
 
-        def scatter(t, pair, first, last):
-            nc.vector.tensor_tensor(
-                windows[t][:].indirect(slots(first, last)), y[t, pair][:], gates[:, first * C : last * C], MULT
-            )
+        def scatter_times_gate(t, first, last, values):
+            nc.vector.tensor_tensor(windows[t][:].indirect(slots(first, last)), values, gate_of(first, last), MULT)
 
-        scatter(0, 0, 0, 2)
-        for t, pair in ((1, 0), (2, 0), (0, 1), (1, 1)):
-            nc.vector.tensor_copy(windows[t][:].indirect(slots(2 * pair, 2 * pair + 2)), y[t, pair])
-        scatter(2, 1, 2, 4)
-        for pair in range(2, 4):
-            for t in range(2):
-                scatter(t, pair, 2 * pair, 2 * pair + 2)
+        def scatter_gated(t, first, last, values):
+            nc.vector.tensor_copy(windows[t][:].indirect(slots(first, last)), values)
+
+        scatter_times_gate(0, 0, 2, y_0_0[:])
+        scatter_gated(1, 0, 2, gated_0[:, 0, :])
+        scatter_gated(2, 0, 2, gated_2_0[:])
+        scatter_gated(0, 2, 4, gated_2[:, 0, :])
+        scatter_gated(1, 2, 4, gated_2[:, 1, :])
+        scatter_times_gate(2, 2, 4, y_2_2)
+        scatter_times_gate(0, 4, 6, y_0_4)
+        scatter_times_gate(1, 4, 6, y_1_4)
+        scatter_times_gate(0, 6, E, y_0_6)
+        scatter_times_gate(1, 6, E, y_1_6)
         for t in range(2):
             nc.sync.dma_start(out[t * P : (t + 1) * P, :], windows[t][:])
-        scatter(2, 2, 4, E)
+        scatter_times_gate(2, 4, E, y_2_4)
         nc.sync.dma_start(out[2 * P :, :], windows[2][:])

@@ -30,8 +30,8 @@ def tile_moe_pkd_glu_silu_kernel(
         keep = ctx.enter_context(tc.tile_pool(name="keep", bufs=1))
         psum = ctx.enter_context(tc.psum_pool(name="psum", bufs=1))
 
-        def held(shape, dtype, name, slot=None):
-            return keep.tile(shape, dtype, name=name, tag=slot or name, align_bytes=64)
+        def held(shape, dtype, name, buffer=None):
+            return keep.tile(shape, dtype, name=name, tag=buffer or name, align_bytes=64)
 
         def banked(shape, name, bank):
             return psum.tile(shape, F32, name=name, tag=f"bank_{bank}")
@@ -111,31 +111,56 @@ def tile_moe_pkd_glu_silu_kernel(
         ident = held([P, P], F32, "ident")
         make_identity(nc, ident[:])
 
-        xg, h, hq = {}, {}, {}
-        xs = held([P, S], U8, "xs")
-        nc.vector.tensor_copy(xs[:], x_plane[:].indirect(offsets[:]))
+        xg, xs, h, hq = {}, {}, {}, {}
+
+        def gather_plane(first, last):
+            plane = held([P, (last - first) * C], U8, f"xs_{first}")
+            nc.vector.tensor_copy(plane[:], x_plane[:].indirect(slots(first, last)))
+            for e in range(first, last):
+                xs[e] = plane[:, (e - first) * C : (e - first + 1) * C]
+
+        nc.vector.memset(windows[0][:], 0.0)
+        gather_plane(0, 2)
+        warm_plane = held([P, H], U8, "warm_plane")
+        nc.vector.memset(warm_plane[:].bitcast(I32), 0)
+        warm_codes = held([P, C], U32, "warm_codes")
+        nc.vector.quantize_mx(
+            out=warm_codes[:].bitcast(FP8X4), scales=warm_plane[:, :C], in_=windows[0][:, : 2 * C].bitcast(BF16)
+        )
+        warm_ps = banked([P, H], "warm_ps", 6)
+        for warm_pass in range(4):
+            nc.tensor.matmul_mx(
+                warm_ps[:],
+                lhsT=warm_codes[:].bitcast(FP8X4),
+                lhsT_scale=xs[0],
+                rhs=w1[0].bitcast(FP4X4),
+                rhs_scale=warm_plane[:],
+                start=True,
+                stop=True,
+            )
+        gather_plane(2, E)
         for first, last in ((0, 2), (2, E)):
             gathered = held([P, (last - first) * C], U32, f"xg_{first}")
             nc.vector.tensor_copy(gathered[:], x_table[:].indirect(slots(first, last)))
             for e in range(first, last):
                 xg[e] = gathered[:, (e - first) * C : (e - first + 1) * C]
 
-        def up(e, a_bank, b_bank, act_slot, h_slot):
+        def up(e, a_bank, b_bank, act_buffer, h_buffer):
             a_ps = banked([P, H], f"a_ps_{e}", a_bank)
             b_ps = banked([P, H], f"b_ps_{e}", b_bank)
             for acc, words, plane in ((a_ps, w1, w1_plane), (b_ps, w3, w3_plane)):
                 nc.tensor.matmul_mx(
                     acc[:],
                     lhsT=xg[e].bitcast(FP8X4),
-                    lhsT_scale=xs[:, e * C : (e + 1) * C],
+                    lhsT_scale=xs[e],
                     rhs=words[e].bitcast(FP4X4),
                     rhs_scale=plane[e],
                     start=True,
                     stop=True,
                 )
-            act = held([P, 2, P, 2], F32, f"act_{e}", act_slot)
+            act = held([P, 2, P, 2], F32, f"act_{e}", act_buffer)
             nc.scalar.activation(act[:], a_ps[:].rearrange("s (q u v) -> s u q v", u=2, v=2), SILU)
-            h[e] = held([P, 2, P, 2], BF16, f"h_{e}", h_slot)
+            h[e] = held([P, 2, P, 2], BF16, f"h_{e}", h_buffer)
             b_view = b_ps[:].rearrange("s (q u v) -> s u q v", u=2, v=2)
             if e < E // 2:
                 nc.vector.tensor_tensor(h[e][:], b_view, act[:], MULT)
@@ -144,23 +169,23 @@ def tile_moe_pkd_glu_silu_kernel(
                 nc.scalar.copy(b_sb[:], b_view)
                 nc.gpsimd.tensor_tensor(h[e][:], b_sb[:], act[:], MULT)
 
-        def turn(e, ht_ps, x):
+        def turn(e, ht_ps, j):
             pairs = h[e][:].rearrange("s u q v -> s (u q v)").bitcast(F32)
             for u in range(2):
-                nc.tensor.transpose(ht_ps[:, x, u, :], pairs[:, u * P : (u + 1) * P], ident[:])
+                nc.tensor.transpose(ht_ps[:, j, u, :], pairs[:, u * P : (u + 1) * P], ident[:])
 
         def quantise(first, last, ht_ps):
             count = last - first
             ht = held([P, count * C * 4], BF16, f"ht_{first}")
             nc.scalar.copy(
-                ht[:].bitcast(F32).rearrange("q (x s u) -> q x s u", x=count, u=2),
-                ht_ps[:].rearrange("q x u s -> q x s u"),
+                ht[:].bitcast(F32).rearrange("q (j s u) -> q j s u", j=count, u=2),
+                ht_ps[:].rearrange("q j u s -> q j s u"),
             )
             codes = held([P, count * C], U32, f"h_codes_{first}")
             plane = held([P, count * C], U8, f"h_plane_{first}")
             nc.vector.quantize_mx(out=codes[:].bitcast(FP8X4), scales=plane[:], in_=ht[:])
-            for x in range(count):
-                hq[first + x] = (codes[:, x * C : (x + 1) * C], plane[:, x * C : (x + 1) * C])
+            for j in range(count):
+                hq[first + j] = (codes[:, j * C : (j + 1) * C], plane[:, j * C : (j + 1) * C])
 
         def down(acc, e, t):
             nc.tensor.matmul_mx(
@@ -173,27 +198,27 @@ def tile_moe_pkd_glu_silu_kernel(
                 stop=True,
             )
 
-        def down_plain(t, first, last, bank, slot=None):
+        def down_plain(t, first, last, bank, buffer=None):
             y_ps = banked([P, (last - first) * C], f"y_ps_{t}_{first}", bank)
             for e in range(first, last):
                 down(y_ps[:, (e - first) * C : (e - first + 1) * C], e, t)
-            y_sb = held([P, (last - first) * C], F32, f"y_{t}_{first}", slot)
+            y_sb = held([P, (last - first) * C], F32, f"y_{t}_{first}", buffer)
             nc.scalar.copy(y_sb[:], y_ps[:])
             return y_sb[:]
 
         def down_gated(row_tiles, first, last, bank):
             shape = [P, len(row_tiles), (last - first) * C]
             y_ps = banked(shape, f"y_ps_{row_tiles[0]}_{first}", bank)
-            for i, t in enumerate(row_tiles):
+            for j, t in enumerate(row_tiles):
                 for e in range(first, last):
-                    down(y_ps[:, i, (e - first) * C : (e - first + 1) * C], e, t)
+                    down(y_ps[:, j, (e - first) * C : (e - first + 1) * C], e, t)
             gated = held(shape, F32, f"gated_{first}")
             nc.vector.tensor_tensor(gated[:], y_ps[:], gate_of(first, last).unsqueeze(1).to_broadcast(shape), MULT)
             return gated
 
         for e in range(2):
             ht_ps = banked([P, 1, 2, C], f"ht_ps_{e}", 4 + e)
-            up(e, a_bank=e, b_bank=2 + e, act_slot=f"act_{e}", h_slot=f"h_{e}")
+            up(e, a_bank=e, b_bank=2 + e, act_buffer=f"act_{e}", h_buffer=f"h_{e}")
             turn(e, ht_ps, 0)
             quantise(e, e + 1, ht_ps)
         y_0_0 = held([P, 2 * C], F32, "y_0_0")
@@ -201,33 +226,33 @@ def tile_moe_pkd_glu_silu_kernel(
             y_ps = banked([P, C], f"y_ps_first_{e}", e)
             down(y_ps[:], e, 0)
             nc.scalar.copy(y_0_0[:, e * C : (e + 1) * C], y_ps[:])
-        gated_0 = down_gated((1,), 0, 2, bank=5)
+        gated_1_0 = down_gated((1,), 0, 2, bank=5)
         y_2_0 = down_plain(2, 0, 2, bank=4)
 
         ht_ps = banked([P, 2, 2, C], "ht_ps_2", 1)
-        up(2, a_bank=6, b_bank=2, act_slot="act_2", h_slot="h_0")
+        up(2, a_bank=6, b_bank=2, act_buffer="act_2", h_buffer="h_0")
         turn(2, ht_ps, 0)
-        up(3, a_bank=7, b_bank=3, act_slot="h_1", h_slot="h_3")
+        up(3, a_bank=7, b_bank=3, act_buffer="h_1", h_buffer="h_3")
         turn(3, ht_ps, 1)
         quantise(2, 4, ht_ps)
 
         gated_2_0 = held([P, 2 * C], F32, "gated_2_0", "ht_2")
         nc.gpsimd.tensor_tensor(gated_2_0[:], y_2_0, gate_of(0, 2), MULT)
 
-        up(4, a_bank=6, b_bank=4, act_slot="act_0", h_slot="h_0")
-        gated_2 = down_gated((0, 1), 2, 4, bank=6)
-        up(5, a_bank=4, b_bank=3, act_slot="act_1", h_slot="h_1")
-        up(6, a_bank=0, b_bank=7, act_slot="act_2", h_slot="h_3")
-        up(7, a_bank=7, b_bank=2, act_slot="act_7", h_slot="h_7")
+        up(4, a_bank=6, b_bank=4, act_buffer="act_0", h_buffer="h_0")
+        gated_01_2 = down_gated((0, 1), 2, 4, bank=6)
+        up(5, a_bank=4, b_bank=3, act_buffer="act_1", h_buffer="h_1")
+        up(6, a_bank=0, b_bank=7, act_buffer="act_2", h_buffer="h_3")
+        up(7, a_bank=7, b_bank=2, act_buffer="act_7", h_buffer="h_7")
 
         ht_ps = banked([P, 2, 2, C], "ht_ps_4", 7)
-        for x in range(2):
-            turn(4 + x, ht_ps, x)
+        for j in range(2):
+            turn(4 + j, ht_ps, j)
         quantise(4, 6, ht_ps)
-        y_2_2 = down_plain(2, 2, 4, bank=2, slot="h_1")
+        y_2_2 = down_plain(2, 2, 4, bank=2, buffer="h_1")
         ht_ps = banked([P, 2, 2, C], "ht_ps_6", 7)
-        for x in range(2):
-            turn(6 + x, ht_ps, x)
+        for j in range(2):
+            turn(6 + j, ht_ps, j)
         quantise(6, E, ht_ps)
 
         y_0_4 = down_plain(0, 4, 6, bank=6)
@@ -236,7 +261,6 @@ def tile_moe_pkd_glu_silu_kernel(
         y_1_6 = down_plain(1, 6, E, bank=0)
         y_2_4 = down_plain(2, 4, E, bank=3)
 
-        nc.vector.memset(windows[0][:], 0.0)
         for window in windows[1:]:
             nc.scalar.copy(window[:, : T - DMA_CLEARED], zero[:, :1].to_broadcast([P, T - DMA_CLEARED]))
 
@@ -247,10 +271,10 @@ def tile_moe_pkd_glu_silu_kernel(
             nc.vector.tensor_copy(windows[t][:].indirect(slots(first, last)), values)
 
         scatter_times_gate(0, 0, 2, y_0_0[:])
-        scatter_gated(1, 0, 2, gated_0[:, 0, :])
+        scatter_gated(1, 0, 2, gated_1_0[:, 0, :])
         scatter_gated(2, 0, 2, gated_2_0[:])
-        scatter_gated(0, 2, 4, gated_2[:, 0, :])
-        scatter_gated(1, 2, 4, gated_2[:, 1, :])
+        scatter_gated(0, 2, 4, gated_01_2[:, 0, :])
+        scatter_gated(1, 2, 4, gated_01_2[:, 1, :])
         scatter_times_gate(2, 2, 4, y_2_2)
         scatter_times_gate(0, 4, 6, y_0_4)
         scatter_times_gate(1, 4, 6, y_1_4)

@@ -37,7 +37,6 @@ def tile_moe_pkd_glu_silu_kernel(
             return psum.tile(shape, F32, name=name, tag=f"bank_{bank}")
 
         offsets = keep.tile([P, S // 16], U16, name="offsets")
-        nc.sync.dma_start(offsets[:], offs)
 
         def slots(first, last):
             return offsets[:, first * C // 16 : last * C // 16]
@@ -83,6 +82,7 @@ def tile_moe_pkd_glu_silu_kernel(
         w1, w3, w2 = {}, {}, {}
         w1_plane, w3_plane, w2_plane = {}, {}, {}
         load_words(w1_words, 0, 2, w1, "w1")
+        nc.sync.dma_start(offsets[:], offs)
         load_scale_rows(x_plane, x_scales.rearrange("o q w -> q o w"))
         x_table = held([P, T], U32, "x_table")
         nc.sync.dma_start(x_table[:].bitcast(I32), x_words[0].rearrange("p t r -> p (t r)").bitcast(I32))
@@ -96,8 +96,8 @@ def tile_moe_pkd_glu_silu_kernel(
         load_gate(0, 2)
         load_plane(w1_scales, 4, E, w1_plane, "w1_plane")
         clear_tail(1)
-        load_plane(w3_scales, 4, E, w3_plane, "w3_plane")
         load_words(w1_words, 4, 6, w1, "w1")
+        load_plane(w3_scales, 4, E, w3_plane, "w3_plane")
         load_words(w3_words, 4, 6, w3, "w3")
         load_words(w2_words, 2, 4, w2, "w2")
         load_gate(2, 4)
@@ -222,27 +222,32 @@ def tile_moe_pkd_glu_silu_kernel(
             turn(e, ht_ps, 0)
             quantise(e, e + 1, ht_ps)
         y_0_0 = held([P, 2 * C], F32, "y_0_0")
+
+        up(2, a_bank=6, b_bank=0, act_buffer="act_2", h_buffer="h_0")
+        up(3, a_bank=7, b_bank=3, act_buffer="act_3", h_buffer="ht_0")
+
+        y_1_ps = banked([P, 2 * C], "y_ps_1_0", 5)
         for e in range(2):
-            y_ps = banked([P, C], f"y_ps_first_{e}", e)
+            y_ps = banked([P, C], f"y_ps_first_{e}", 2 - e)
             down(y_ps[:], e, 0)
+            down(y_1_ps[:, e * C : (e + 1) * C], e, 1)
             nc.scalar.copy(y_0_0[:, e * C : (e + 1) * C], y_ps[:])
-        gated_1_0 = down_gated((1,), 0, 2, bank=5)
+        gated_1_0 = held([P, 2 * C], F32, "gated_1_0")
+        nc.vector.tensor_tensor(gated_1_0[:], y_1_ps[:], gate_of(0, 2), MULT)
         y_2_0 = down_plain(2, 0, 2, bank=4)
 
         ht_ps = banked([P, 2, 2, C], "ht_ps_2", 1)
-        up(2, a_bank=6, b_bank=2, act_buffer="act_2", h_buffer="h_0")
-        turn(2, ht_ps, 0)
-        up(3, a_bank=7, b_bank=3, act_buffer="h_1", h_buffer="h_3")
-        turn(3, ht_ps, 1)
+        for j in range(2):
+            turn(2 + j, ht_ps, j)
         quantise(2, 4, ht_ps)
 
         gated_2_0 = held([P, 2 * C], F32, "gated_2_0", "ht_2")
         nc.gpsimd.tensor_tensor(gated_2_0[:], y_2_0, gate_of(0, 2), MULT)
 
         up(4, a_bank=6, b_bank=4, act_buffer="act_0", h_buffer="h_0")
-        gated_01_2 = down_gated((0, 1), 2, 4, bank=6)
+        gated_01_2 = down_gated((0, 1), 2, 4, bank=5)
         up(5, a_bank=4, b_bank=3, act_buffer="act_1", h_buffer="h_1")
-        up(6, a_bank=0, b_bank=7, act_buffer="act_2", h_buffer="h_3")
+        up(6, a_bank=0, b_bank=7, act_buffer="act_2", h_buffer="ht_0")
         up(7, a_bank=7, b_bank=2, act_buffer="act_7", h_buffer="h_7")
 
         ht_ps = banked([P, 2, 2, C], "ht_ps_4", 7)
@@ -271,7 +276,7 @@ def tile_moe_pkd_glu_silu_kernel(
             nc.vector.tensor_copy(windows[t][:].indirect(slots(first, last)), values)
 
         scatter_times_gate(0, 0, 2, y_0_0[:])
-        scatter_gated(1, 0, 2, gated_1_0[:, 0, :])
+        scatter_gated(1, 0, 2, gated_1_0[:])
         scatter_gated(2, 0, 2, gated_2_0[:])
         scatter_gated(0, 2, 4, gated_01_2[:, 0, :])
         scatter_gated(1, 2, 4, gated_01_2[:, 1, :])

@@ -41,18 +41,22 @@ def tile_moe_pkd_glu_silu_kernel(
         def slots(first, last):
             return offsets[:, first * C // 16 : last * C // 16]
 
-        def load_scale_rows(plane, scales):
+        def load_scale_rows(plane, scales, rows=range(4), queue=nc.sync):
             by_row = scales.rearrange("(q r) e w -> r q e w", r=4)
             as_int = plane[:].bitcast(I32)
-            for r in range(4):
-                nc.sync.dma_start(
+            for r in rows:
+                queue.dma_start(
                     as_int[r:P:32, :].rearrange("q (e w) -> q e w", e=scales.shape[1]), by_row[r].bitcast(I32)
                 )
 
-        def load_plane(scales, first, last, planes, name):
+        plane_tiles = {}
+
+        def load_plane(scales, first, last, planes, name, rows=range(4), queue=nc.sync):
             width = scales.shape[3]
-            plane = held([P, (last - first) * width], U8, f"{name}_{first}")
-            load_scale_rows(plane, scales[first:last].rearrange("e s q w -> q (e s) w"))
+            if (name, first) not in plane_tiles:
+                plane_tiles[(name, first)] = held([P, (last - first) * width], U8, f"{name}_{first}")
+            plane = plane_tiles[(name, first)]
+            load_scale_rows(plane, scales[first:last].rearrange("e s q w -> q (e s) w"), rows, queue)
             for e in range(first, last):
                 planes[e] = plane[:, (e - first) * width : (e - first + 1) * width]
 
@@ -94,19 +98,19 @@ def tile_moe_pkd_glu_silu_kernel(
         load_plane(w2_scales, 0, 4, w2_plane, "w2_plane")
         load_words(w2_words, 0, 2, w2, "w2")
         load_gate(0, 2)
-        load_plane(w1_scales, 4, E, w1_plane, "w1_plane")
+        load_plane(w1_scales, 4, 8, w1_plane, "w1_plane")
         clear_tail(1)
         load_words(w1_words, 4, 6, w1, "w1")
-        load_plane(w3_scales, 4, E, w3_plane, "w3_plane")
+        load_plane(w3_scales, 4, 8, w3_plane, "w3_plane")
         load_words(w3_words, 4, 6, w3, "w3")
+        clear_tail(2)
+        load_words(w1_words, 6, 8, w1, "w1")
+        load_words(w3_words, 6, 8, w3, "w3")
         load_words(w2_words, 2, 4, w2, "w2")
         load_gate(2, 4)
-        clear_tail(2)
-        load_words(w1_words, 6, E, w1, "w1")
-        load_words(w3_words, 6, E, w3, "w3")
-        load_plane(w2_scales, 4, E, w2_plane, "w2_plane")
-        load_words(w2_words, 4, E, w2, "w2")
-        load_gate(4, E)
+        load_plane(w2_scales, 4, 8, w2_plane, "w2_plane")
+        load_words(w2_words, 4, 8, w2, "w2")
+        load_gate(4, 8)
 
         ident = held([P, P], F32, "ident")
         make_identity(nc, ident[:])
@@ -212,7 +216,7 @@ def tile_moe_pkd_glu_silu_kernel(
             for j, t in enumerate(row_tiles):
                 for e in range(first, last):
                     down(y_ps[:, j, (e - first) * C : (e - first + 1) * C], e, t)
-            gated = held(shape, F32, f"gated_{first}")
+            gated = held(shape, F32, f"gated_{row_tiles[0]}_{first}")
             nc.vector.tensor_tensor(gated[:], y_ps[:], gate_of(first, last).unsqueeze(1).to_broadcast(shape), MULT)
             return gated
 
@@ -223,12 +227,12 @@ def tile_moe_pkd_glu_silu_kernel(
             quantise(e, e + 1, ht_ps)
         y_0_0 = held([P, 2 * C], F32, "y_0_0")
 
-        up(2, a_bank=6, b_bank=0, act_buffer="act_2", h_buffer="h_0")
+        up(2, a_bank=6, b_bank=2, act_buffer="act_2", h_buffer="h_0")
         up(3, a_bank=7, b_bank=3, act_buffer="act_3", h_buffer="ht_0")
 
         y_1_ps = banked([P, 2 * C], "y_ps_1_0", 5)
         for e in range(2):
-            y_ps = banked([P, C], f"y_ps_first_{e}", 2 - e)
+            y_ps = banked([P, C], f"y_ps_first_{e}", e)
             down(y_ps[:], e, 0)
             down(y_1_ps[:, e * C : (e + 1) * C], e, 1)
             nc.scalar.copy(y_0_0[:, e * C : (e + 1) * C], y_ps[:])
@@ -245,23 +249,24 @@ def tile_moe_pkd_glu_silu_kernel(
         nc.gpsimd.tensor_tensor(gated_2_0[:], y_2_0, gate_of(0, 2), MULT)
 
         up(4, a_bank=6, b_bank=4, act_buffer="act_0", h_buffer="h_0")
-        gated_01_2 = down_gated((0, 1), 2, 4, bank=5)
-        up(5, a_bank=4, b_bank=3, act_buffer="act_1", h_buffer="h_1")
-        up(6, a_bank=0, b_bank=7, act_buffer="act_2", h_buffer="ht_0")
-        up(7, a_bank=7, b_bank=2, act_buffer="act_7", h_buffer="h_7")
+        gated_0_2 = down_gated((0,), 2, 4, bank=6)
+        gated_1_2 = down_gated((1,), 2, 4, bank=4)
+        up(5, a_bank=7, b_bank=3, act_buffer="w3_4", h_buffer="h_1")
+        up(6, a_bank=0, b_bank=2, act_buffer="act_2", h_buffer="ht_0")
+        up(7, a_bank=5, b_bank=1, act_buffer="act_7", h_buffer="h_7")
 
-        ht_ps = banked([P, 2, 2, C], "ht_ps_4", 7)
+        ht_ps = banked([P, 2, 2, C], "ht_ps_4", 5)
         for j in range(2):
             turn(4 + j, ht_ps, j)
         quantise(4, 6, ht_ps)
-        y_2_2 = down_plain(2, 2, 4, bank=2, buffer="h_1")
-        ht_ps = banked([P, 2, 2, C], "ht_ps_6", 7)
+        y_2_2 = down_plain(2, 2, 4, bank=7, buffer="h_1")
+        ht_ps = banked([P, 2, 2, C], "ht_ps_6", 5)
         for j in range(2):
             turn(6 + j, ht_ps, j)
         quantise(6, E, ht_ps)
 
         y_0_4 = down_plain(0, 4, 6, bank=6)
-        y_1_4 = down_plain(1, 4, 6, bank=5)
+        y_1_4 = down_plain(1, 4, 6, bank=1)
         y_0_6 = down_plain(0, 6, E, bank=4)
         y_1_6 = down_plain(1, 6, E, bank=0)
         y_2_4 = down_plain(2, 4, E, bank=3)
@@ -278,8 +283,8 @@ def tile_moe_pkd_glu_silu_kernel(
         scatter_times_gate(0, 0, 2, y_0_0[:])
         scatter_gated(1, 0, 2, gated_1_0[:])
         scatter_gated(2, 0, 2, gated_2_0[:])
-        scatter_gated(0, 2, 4, gated_01_2[:, 0, :])
-        scatter_gated(1, 2, 4, gated_01_2[:, 1, :])
+        scatter_gated(0, 2, 4, gated_0_2[:, 0, :])
+        scatter_gated(1, 2, 4, gated_1_2[:, 0, :])
         scatter_times_gate(2, 2, 4, y_2_2)
         scatter_times_gate(0, 4, 6, y_0_4)
         scatter_times_gate(1, 4, 6, y_1_4)

@@ -85,11 +85,13 @@ def tile_moe_pkd_glu_silu_kernel(
 
         w1, w3, w2 = {}, {}, {}
         w1_plane, w3_plane, w2_plane = {}, {}, {}
+        x_table = held([P, T], U32, "x_table")
+        x_int = x_words[0].rearrange("p t r -> p (t r)").bitcast(I32)
+        nc.sync.dma_start(x_table[:, :C].bitcast(I32), x_int[:, :C])
         load_words(w1_words, 0, 2, w1, "w1")
         nc.sync.dma_start(offsets[:], offs)
         load_scale_rows(x_plane, x_scales.rearrange("o q w -> q o w"))
-        x_table = held([P, T], U32, "x_table")
-        nc.sync.dma_start(x_table[:].bitcast(I32), x_words[0].rearrange("p t r -> p (t r)").bitcast(I32))
+        nc.sync.dma_start(x_table[:, C:].bitcast(I32), x_int[:, C:])
         load_plane(w1_scales, 0, 4, w1_plane, "w1_plane")
         load_words(w3_words, 0, 2, w3, "w3")
         load_plane(w3_scales, 0, 4, w3_plane, "w3_plane")
@@ -122,23 +124,20 @@ def tile_moe_pkd_glu_silu_kernel(
             nc.vector.tensor_copy(plane[:], x_plane[:].indirect(slots(first, last)))
             for e in range(first, last):
                 xs[e] = plane[:, (e - first) * C : (e - first + 1) * C]
+            return plane[:]
 
         nc.vector.memset(windows[0][:], 0.0)
-        gather_plane(0, 2)
-        warm_plane = held([P, H], U8, "warm_plane")
-        nc.vector.memset(warm_plane[:].bitcast(I32), 0)
+        first_bytes = gather_plane(0, 2)
         warm_codes = held([P, C], U32, "warm_codes")
-        nc.vector.quantize_mx(
-            out=warm_codes[:].bitcast(FP8X4), scales=warm_plane[:, :C], in_=windows[0][:, : 2 * C].bitcast(BF16)
-        )
-        warm_ps = banked([P, H], "warm_ps", 6)
-        for warm_pass in range(4):
+        nc.vector.tensor_copy(warm_codes[:], x_table[:, :C])
+        warm_ps = banked([P, 2 * C], "warm_ps", 6)
+        for warm_pass in range(5):
             nc.tensor.matmul_mx(
                 warm_ps[:],
                 lhsT=warm_codes[:].bitcast(FP8X4),
                 lhsT_scale=xs[0],
-                rhs=w1[0].bitcast(FP4X4),
-                rhs_scale=warm_plane[:],
+                rhs=w1[0][:, : 4 * C].bitcast(FP4X4),
+                rhs_scale=first_bytes,
                 start=True,
                 stop=True,
             )

@@ -100,49 +100,48 @@ def tile_moe_pkd_glu_silu_kernel(
         load_plane(w2_scales, 0, 4, w2_plane, "w2_plane")
         load_words(w2_words, 0, 2, w2, "w2")
         load_gate(0, 2)
-        load_plane(w1_scales, 4, 8, w1_plane, "w1_plane")
+        load_plane(w1_scales, 4, 8, w1_plane, "w1_plane", rows=range(2))
         clear_tail(1)
+        load_plane(w1_scales, 4, 8, w1_plane, "w1_plane", rows=range(2, 4))
         load_words(w1_words, 4, 6, w1, "w1")
         load_plane(w3_scales, 4, 8, w3_plane, "w3_plane")
         load_words(w3_words, 4, 6, w3, "w3")
-        clear_tail(2)
         load_words(w1_words, 6, 8, w1, "w1")
         load_words(w3_words, 6, 8, w3, "w3")
         load_words(w2_words, 2, 4, w2, "w2")
-        load_gate(2, 4)
+        load_gate(2, 8)
         load_plane(w2_scales, 4, 8, w2_plane, "w2_plane")
         load_words(w2_words, 4, 8, w2, "w2")
-        load_gate(4, 8)
 
         ident = held([P, P], F32, "ident")
         make_identity(nc, ident[:])
 
         xg, xs, h, hq = {}, {}, {}, {}
 
+        slot_plane = held([P, S], U8, "slot_plane")
+        xs.update({e: slot_plane[:, e * C : (e + 1) * C] for e in range(E)})
+
         def gather_plane(first, last):
-            plane = held([P, (last - first) * C], U8, f"xs_{first}")
-            nc.vector.tensor_copy(plane[:], x_plane[:].indirect(slots(first, last)))
-            for e in range(first, last):
-                xs[e] = plane[:, (e - first) * C : (e - first + 1) * C]
-            return plane[:]
+            nc.vector.tensor_copy(slot_plane[:, first * C : last * C], x_plane[:].indirect(slots(first, last)))
 
         nc.vector.memset(windows[0][:], 0.0)
-        first_bytes = gather_plane(0, 2)
+        gather_plane(0, 2)
+        gather_plane(2, 4)
         warm_codes = held([P, C], U32, "warm_codes")
         nc.vector.tensor_copy(warm_codes[:], x_table[:, :C])
-        warm_ps = banked([P, 2 * C], "warm_ps", 6)
-        for warm_pass in range(5):
+        warm_ps = banked([P, H], "warm_ps", 6)
+        for width in (2 * C, 2 * C, H, H, H):
             nc.tensor.matmul_mx(
-                warm_ps[:],
+                warm_ps[:, :width],
                 lhsT=warm_codes[:].bitcast(FP8X4),
                 lhsT_scale=xs[0],
-                rhs=w1[0][:, : 4 * C].bitcast(FP4X4),
-                rhs_scale=first_bytes,
+                rhs=w1[0][:, : 2 * width].bitcast(FP4X4),
+                rhs_scale=slot_plane[:, :width],
                 start=True,
                 stop=True,
             )
-        gather_plane(2, E)
-        for first, last in ((0, 2), (2, E)):
+        gather_plane(4, E)
+        for first, last in ((0, 2), (2, 4), (4, E)):
             gathered = held([P, (last - first) * C], U32, f"xg_{first}")
             nc.vector.tensor_copy(gathered[:], x_table[:].indirect(slots(first, last)))
             for e in range(first, last):
@@ -270,8 +269,8 @@ def tile_moe_pkd_glu_silu_kernel(
         y_1_6 = down_plain(1, 6, E, bank=0)
         y_2_4 = down_plain(2, 4, E, bank=3)
 
-        for window in windows[1:]:
-            nc.scalar.copy(window[:, : T - DMA_CLEARED], zero[:, :1].to_broadcast([P, T - DMA_CLEARED]))
+        for window, width in ((windows[1], T - DMA_CLEARED), (windows[2], T)):
+            nc.scalar.copy(window[:, :width], zero[:, :1].to_broadcast([P, width]))
 
         def scatter_times_gate(t, first, last, values):
             nc.vector.tensor_tensor(windows[t][:].indirect(slots(first, last)), values, gate_of(first, last), MULT)

@@ -41,22 +41,22 @@ def tile_moe_pkd_glu_silu_kernel(
         def slots(first, last):
             return offsets[:, first * C // 16 : last * C // 16]
 
-        def load_scale_rows(plane, scales, rows=range(4), queue=nc.sync):
+        def load_scale_rows(plane, scales, rows=range(4)):
             by_row = scales.rearrange("(q r) e w -> r q e w", r=4)
             as_int = plane[:].bitcast(I32)
             for r in rows:
-                queue.dma_start(
+                nc.sync.dma_start(
                     as_int[r:P:32, :].rearrange("q (e w) -> q e w", e=scales.shape[1]), by_row[r].bitcast(I32)
                 )
 
         plane_tiles = {}
 
-        def load_plane(scales, first, last, planes, name, rows=range(4), queue=nc.sync):
+        def load_plane(scales, first, last, planes, name, rows=range(4)):
             width = scales.shape[3]
             if (name, first) not in plane_tiles:
                 plane_tiles[(name, first)] = held([P, (last - first) * width], U8, f"{name}_{first}")
             plane = plane_tiles[(name, first)]
-            load_scale_rows(plane, scales[first:last].rearrange("e s q w -> q (e s) w"), rows, queue)
+            load_scale_rows(plane, scales[first:last].rearrange("e s q w -> q (e s) w"), rows)
             for e in range(first, last):
                 planes[e] = plane[:, (e - first) * width : (e - first + 1) * width]
 
@@ -80,9 +80,6 @@ def tile_moe_pkd_glu_silu_kernel(
         nc.vector.memset(zero[:], 0.0)
         windows = [keep.tile([P, T], F32, name=f"window_{t}") for t in range(N // P)]
 
-        def clear_tail(t):
-            nc.sync.dma_start(windows[t][:, T - DMA_CLEARED :], zero[:])
-
         w1, w3, w2 = {}, {}, {}
         w1_plane, w3_plane, w2_plane = {}, {}, {}
         x_table = held([P, T], U32, "x_table")
@@ -101,7 +98,7 @@ def tile_moe_pkd_glu_silu_kernel(
         load_words(w2_words, 0, 2, w2, "w2")
         load_gate(0, 2)
         load_plane(w1_scales, 4, 8, w1_plane, "w1_plane", rows=range(2))
-        clear_tail(1)
+        nc.sync.dma_start(windows[1][:, T - DMA_CLEARED :], zero[:])
         load_plane(w1_scales, 4, 8, w1_plane, "w1_plane", rows=range(2, 4))
         load_words(w1_words, 4, 6, w1, "w1")
         load_plane(w3_scales, 4, 8, w3_plane, "w3_plane")
@@ -116,10 +113,9 @@ def tile_moe_pkd_glu_silu_kernel(
         ident = held([P, P], F32, "ident")
         make_identity(nc, ident[:])
 
-        xg, xs, h, hq = {}, {}, {}, {}
-
+        xg, h, hq = {}, {}, {}
         slot_plane = held([P, S], U8, "slot_plane")
-        xs.update({e: slot_plane[:, e * C : (e + 1) * C] for e in range(E)})
+        xs = [slot_plane[:, e * C : (e + 1) * C] for e in range(E)]
 
         def gather_plane(first, last):
             nc.vector.tensor_copy(slot_plane[:, first * C : last * C], x_plane[:].indirect(slots(first, last)))
@@ -270,7 +266,7 @@ def tile_moe_pkd_glu_silu_kernel(
         y_2_4 = down_plain(2, 4, E, bank=3)
 
         for window, width in ((windows[1], T - DMA_CLEARED), (windows[2], T)):
-            nc.scalar.copy(window[:, :width], zero[:, :1].to_broadcast([P, width]))
+            nc.scalar.activation(window[:, :width], zero[:, :1].to_broadcast([P, width]), SILU)
 
         def scatter_times_gate(t, first, last, values):
             nc.vector.tensor_tensor(windows[t][:].indirect(slots(first, last)), values, gate_of(first, last), MULT)

@@ -18,8 +18,7 @@ FP8X4 = mybir.dt.float8_e4m3fn_x4
 FP4X4 = mybir.dt.float4_e2m1fn_x4
 MULT = mybir.AluOpType.mult
 SILU = mybir.ActivationFunctionType.Silu
-
-DMA_CLEARED = 64
+COPY = mybir.ActivationFunctionType.Copy
 
 
 def tile_moe_pkd_glu_silu_kernel(
@@ -41,22 +40,19 @@ def tile_moe_pkd_glu_silu_kernel(
         def slots(first, last):
             return offsets[:, first * C // 16 : last * C // 16]
 
-        def load_scale_rows(plane, scales, rows=range(4)):
+        def load_scale_rows(plane, scales, on_gpsimd=0):
             by_row = scales.rearrange("(q r) e w -> r q e w", r=4)
             as_int = plane[:].bitcast(I32)
-            for r in rows:
-                nc.sync.dma_start(
+            for r in range(4):
+                queue = nc.gpsimd if r >= 4 - on_gpsimd else nc.sync
+                queue.dma_start(
                     as_int[r:P:32, :].rearrange("q (e w) -> q e w", e=scales.shape[1]), by_row[r].bitcast(I32)
                 )
 
-        plane_tiles = {}
-
-        def load_plane(scales, first, last, planes, name, rows=range(4)):
+        def load_plane(scales, first, last, planes, name, on_gpsimd=0, buffer=None):
             width = scales.shape[3]
-            if (name, first) not in plane_tiles:
-                plane_tiles[(name, first)] = held([P, (last - first) * width], U8, f"{name}_{first}")
-            plane = plane_tiles[(name, first)]
-            load_scale_rows(plane, scales[first:last].rearrange("e s q w -> q (e s) w"), rows)
+            plane = held([P, (last - first) * width], U8, f"{name}_{first}", buffer)
+            load_scale_rows(plane, scales[first:last].rearrange("e s q w -> q (e s) w"), on_gpsimd)
             for e in range(first, last):
                 planes[e] = plane[:, (e - first) * width : (e - first + 1) * width]
 
@@ -76,7 +72,7 @@ def tile_moe_pkd_glu_silu_kernel(
 
         x_plane = held([P, T], U8, "x_plane")
         nc.vector.memset(x_plane[:].bitcast(I32), 0)
-        zero = held([P, DMA_CLEARED], F32, "zero")
+        zero = held([P, 1], F32, "zero")
         nc.vector.memset(zero[:], 0.0)
         windows = [keep.tile([P, T], F32, name=f"window_{t}") for t in range(N // P)]
 
@@ -84,49 +80,42 @@ def tile_moe_pkd_glu_silu_kernel(
         w1_plane, w3_plane, w2_plane = {}, {}, {}
         x_table = held([P, T], U32, "x_table")
         x_int = x_words[0].rearrange("p t r -> p (t r)").bitcast(I32)
-        nc.sync.dma_start(x_table[:, :C].bitcast(I32), x_int[:, :C])
+        nc.scalar.dma_start(x_table[:, :C].bitcast(I32), x_int[:, :C])
         load_words(w1_words, 0, 2, w1, "w1")
         nc.sync.dma_start(offsets[:], offs)
         load_scale_rows(x_plane, x_scales.rearrange("o q w -> q o w"))
         nc.sync.dma_start(x_table[:, C:].bitcast(I32), x_int[:, C:])
-        load_plane(w1_scales, 0, 4, w1_plane, "w1_plane")
+        load_plane(w1_scales, 0, E, w1_plane, "w1_plane")
         load_words(w3_words, 0, 2, w3, "w3")
-        load_plane(w3_scales, 0, 4, w3_plane, "w3_plane")
+        load_plane(w3_scales, 0, 4, w3_plane, "w3_plane", on_gpsimd=3)
         load_words(w1_words, 2, 4, w1, "w1")
         load_words(w3_words, 2, 4, w3, "w3")
-        load_plane(w2_scales, 0, 4, w2_plane, "w2_plane")
-        load_words(w2_words, 0, 2, w2, "w2")
-        load_gate(0, 2)
-        load_plane(w1_scales, 4, 8, w1_plane, "w1_plane", rows=range(2))
-        nc.sync.dma_start(windows[1][:, T - DMA_CLEARED :], zero[:])
-        load_plane(w1_scales, 4, 8, w1_plane, "w1_plane", rows=range(2, 4))
         load_words(w1_words, 4, 6, w1, "w1")
         load_plane(w3_scales, 4, 8, w3_plane, "w3_plane")
         load_words(w3_words, 4, 6, w3, "w3")
         load_words(w1_words, 6, 8, w1, "w1")
         load_words(w3_words, 6, 8, w3, "w3")
-        load_words(w2_words, 2, 4, w2, "w2")
-        load_gate(2, 8)
-        load_plane(w2_scales, 4, 8, w2_plane, "w2_plane")
+        load_plane(w2_scales, 0, 8, w2_plane, "w2_plane")
+        load_words(w2_words, 0, 4, w2, "w2")
         load_words(w2_words, 4, 8, w2, "w2")
+        load_gate(0, 4)
+        load_gate(4, 8)
 
         ident = held([P, P], F32, "ident")
         make_identity(nc, ident[:])
 
+        nc.vector.memset(windows[0][:], 0.0)
+        for window in windows[1:]:
+            nc.scalar.activation(window[:], zero[:].to_broadcast([P, T]), SILU)
+
         xg, h, hq = {}, {}, {}
         slot_plane = held([P, S], U8, "slot_plane")
         xs = [slot_plane[:, e * C : (e + 1) * C] for e in range(E)]
-
-        def gather_plane(first, last):
-            nc.vector.tensor_copy(slot_plane[:, first * C : last * C], x_plane[:].indirect(slots(first, last)))
-
-        nc.vector.memset(windows[0][:], 0.0)
-        gather_plane(0, 2)
-        gather_plane(2, 4)
         warm_codes = held([P, C], U32, "warm_codes")
         nc.vector.tensor_copy(warm_codes[:], x_table[:, :C])
-        warm_ps = banked([P, H], "warm_ps", 6)
-        for width in (2 * C, 2 * C, H, H, H):
+        nc.vector.tensor_copy(slot_plane[:, : 4 * C], x_plane[:].indirect(slots(0, 4)))
+        warm_ps = banked([P, H], "warm_ps", 7)
+        for width in (H, H, 64):
             nc.tensor.matmul_mx(
                 warm_ps[:, :width],
                 lhsT=warm_codes[:].bitcast(FP8X4),
@@ -136,16 +125,16 @@ def tile_moe_pkd_glu_silu_kernel(
                 start=True,
                 stop=True,
             )
-        gather_plane(4, E)
+        nc.vector.tensor_copy(slot_plane[:, 4 * C :], x_plane[:].indirect(slots(4, E)))
         for first, last in ((0, 2), (2, 4), (4, E)):
             gathered = held([P, (last - first) * C], U32, f"xg_{first}")
             nc.vector.tensor_copy(gathered[:], x_table[:].indirect(slots(first, last)))
             for e in range(first, last):
                 xg[e] = gathered[:, (e - first) * C : (e - first + 1) * C]
 
-        def up(e, a_bank, b_bank, act_buffer, h_buffer):
-            a_ps = banked([P, H], f"a_ps_{e}", a_bank)
-            b_ps = banked([P, H], f"b_ps_{e}", b_bank)
+        def up(e):
+            a_ps = banked([P, H], f"a_ps_{e}", e % 3)
+            b_ps = banked([P, H], f"b_ps_{e}", 4 + e % 4)
             for acc, words, plane in ((a_ps, w1, w1_plane), (b_ps, w3, w3_plane)):
                 nc.tensor.matmul_mx(
                     acc[:],
@@ -156,135 +145,86 @@ def tile_moe_pkd_glu_silu_kernel(
                     start=True,
                     stop=True,
                 )
-            act = held([P, 2, P, 2], F32, f"act_{e}", act_buffer)
+            act = held([P, 2, P, 2], F32, f"act_{e}")
             nc.scalar.activation(act[:], a_ps[:].rearrange("s (q u v) -> s u q v", u=2, v=2), SILU)
-            h[e] = held([P, 2, P, 2], BF16, f"h_{e}", h_buffer)
-            b_view = b_ps[:].rearrange("s (q u v) -> s u q v", u=2, v=2)
-            if e < E // 2:
-                nc.vector.tensor_tensor(h[e][:], b_view, act[:], MULT)
-            else:
-                b_sb = held([P, 2, P, 2], F32, f"b_sb_{e}")
-                nc.scalar.copy(b_sb[:], b_view)
-                nc.gpsimd.tensor_tensor(h[e][:], b_sb[:], act[:], MULT)
+            h[e] = held([P, 2, P, 2], BF16, f"h_{e}")
+            nc.vector.tensor_tensor(h[e][:], b_ps[:].rearrange("s (q u v) -> s u q v", u=2, v=2), act[:], MULT)
 
-        def turn(e, ht_ps, j):
-            pairs = h[e][:].rearrange("s u q v -> s (u q v)").bitcast(F32)
-            for u in range(2):
-                nc.tensor.transpose(ht_ps[:, j, u, :], pairs[:, u * P : (u + 1) * P], ident[:])
-
-        def quantise(first, last, ht_ps):
-            count = last - first
-            ht = held([P, count * C * 4], BF16, f"ht_{first}")
+        def quantise(first, bank, buffer=None):
+            ht_ps = banked([P, 2, 2, C], f"ht_ps_{first}", bank)
+            for j in range(2):
+                pairs = h[first + j][:].rearrange("s u q v -> s (u q v)").bitcast(F32)
+                for u in range(2):
+                    nc.tensor.transpose(ht_ps[:, j, u, :], pairs[:, u * P : (u + 1) * P], ident[:])
+            ht = held([P, 2 * C * 4], BF16, f"ht_{first}")
             nc.scalar.copy(
-                ht[:].bitcast(F32).rearrange("q (j s u) -> q j s u", j=count, u=2),
+                ht[:].bitcast(F32).rearrange("q (j s u) -> q j s u", j=2, u=2),
                 ht_ps[:].rearrange("q j u s -> q j s u"),
             )
-            codes = held([P, count * C], U32, f"h_codes_{first}")
-            plane = held([P, count * C], U8, f"h_plane_{first}")
+            codes = held([P, 2 * C], U32, f"h_codes_{first}", buffer)
+            plane = held([P, 2 * C], U8, f"h_plane_{first}")
             nc.vector.quantize_mx(out=codes[:].bitcast(FP8X4), scales=plane[:], in_=ht[:])
-            for j in range(count):
+            for j in range(2):
                 hq[first + j] = (codes[:, j * C : (j + 1) * C], plane[:, j * C : (j + 1) * C])
 
-        def down(acc, e, t):
-            nc.tensor.matmul_mx(
-                acc,
-                lhsT=w2[e][:, 2 * t * P : 2 * (t + 1) * P].bitcast(FP4X4),
-                lhsT_scale=w2_plane[e][:, t * P : (t + 1) * P],
-                rhs=hq[e][0].bitcast(FP8X4),
-                rhs_scale=hq[e][1],
-                start=True,
-                stop=True,
-            )
-
-        def down_plain(t, first, last, bank, buffer=None):
+        def down(t, first, last, bank):
             y_ps = banked([P, (last - first) * C], f"y_ps_{t}_{first}", bank)
             for e in range(first, last):
-                down(y_ps[:, (e - first) * C : (e - first + 1) * C], e, t)
+                nc.tensor.matmul_mx(
+                    y_ps[:, (e - first) * C : (e - first + 1) * C],
+                    lhsT=w2[e][:, 2 * t * P : 2 * (t + 1) * P].bitcast(FP4X4),
+                    lhsT_scale=w2_plane[e][:, t * P : (t + 1) * P],
+                    rhs=hq[e][0].bitcast(FP8X4),
+                    rhs_scale=hq[e][1],
+                    start=True,
+                    stop=True,
+                )
+            return y_ps
+
+        def down_plain(t, first, last, bank, buffer=None):
+            y_ps = down(t, first, last, bank)
             y_sb = held([P, (last - first) * C], F32, f"y_{t}_{first}", buffer)
             nc.scalar.copy(y_sb[:], y_ps[:])
-            return y_sb[:]
+            return y_sb
 
-        def down_gated(row_tiles, first, last, bank):
-            shape = [P, len(row_tiles), (last - first) * C]
-            y_ps = banked(shape, f"y_ps_{row_tiles[0]}_{first}", bank)
-            for j, t in enumerate(row_tiles):
-                for e in range(first, last):
-                    down(y_ps[:, j, (e - first) * C : (e - first + 1) * C], e, t)
-            gated = held(shape, F32, f"gated_{row_tiles[0]}_{first}")
-            nc.vector.tensor_tensor(gated[:], y_ps[:], gate_of(first, last).unsqueeze(1).to_broadcast(shape), MULT)
-            return gated
+        def down_gated(t, first, last, bank, into):
+            y_ps = down(t, first, last, bank)
+            nc.vector.tensor_tensor(into[:, first * C : last * C], y_ps[:], gate_of(first, last), MULT)
 
-        for e in range(2):
-            ht_ps = banked([P, 1, 2, C], f"ht_ps_{e}", 4 + e)
-            up(e, a_bank=e, b_bank=2 + e, act_buffer=f"act_{e}", h_buffer=f"h_{e}")
-            turn(e, ht_ps, 0)
-            quantise(e, e + 1, ht_ps)
-        y_0_0 = held([P, 2 * C], F32, "y_0_0")
+        def scatter_on_vector(t, first, last, values):
+            nc.vector.tensor_tensor(windows[t][:].indirect(slots(first, last)), values[:], gate_of(first, last), MULT)
 
-        up(2, a_bank=6, b_bank=2, act_buffer="act_2", h_buffer="h_0")
-        up(3, a_bank=7, b_bank=3, act_buffer="act_3", h_buffer="ht_0")
+        def scatter_on_scalar(t, first, last, gated):
+            nc.scalar.activation(windows[t][:].indirect(offsets[:, first // 16 : last // 16]), gated[:, first:last], COPY)
 
-        y_1_ps = banked([P, 2 * C], "y_ps_1_0", 5)
-        for e in range(2):
-            y_ps = banked([P, C], f"y_ps_first_{e}", e)
-            down(y_ps[:], e, 0)
-            down(y_1_ps[:, e * C : (e + 1) * C], e, 1)
-            nc.scalar.copy(y_0_0[:, e * C : (e + 1) * C], y_ps[:])
-        gated_1_0 = held([P, 2 * C], F32, "gated_1_0")
-        nc.vector.tensor_tensor(gated_1_0[:], y_1_ps[:], gate_of(0, 2), MULT)
-        y_2_0 = down_plain(2, 0, 2, bank=4)
-
-        ht_ps = banked([P, 2, 2, C], "ht_ps_2", 1)
-        for j in range(2):
-            turn(2 + j, ht_ps, j)
-        quantise(2, 4, ht_ps)
-
-        gated_2_0 = held([P, 2 * C], F32, "gated_2_0", "ht_2")
-        nc.gpsimd.tensor_tensor(gated_2_0[:], y_2_0, gate_of(0, 2), MULT)
-
-        up(4, a_bank=6, b_bank=4, act_buffer="act_0", h_buffer="h_0")
-        gated_0_2 = down_gated((0,), 2, 4, bank=6)
-        gated_1_2 = down_gated((1,), 2, 4, bank=4)
-        up(5, a_bank=7, b_bank=3, act_buffer="w3_4", h_buffer="h_1")
-        up(6, a_bank=0, b_bank=2, act_buffer="act_2", h_buffer="ht_0")
-        up(7, a_bank=5, b_bank=1, act_buffer="act_7", h_buffer="h_7")
-
-        ht_ps = banked([P, 2, 2, C], "ht_ps_4", 5)
-        for j in range(2):
-            turn(4 + j, ht_ps, j)
-        quantise(4, 6, ht_ps)
-        y_2_2 = down_plain(2, 2, 4, bank=7, buffer="h_1")
-        ht_ps = banked([P, 2, 2, C], "ht_ps_6", 5)
-        for j in range(2):
-            turn(6 + j, ht_ps, j)
-        quantise(6, E, ht_ps)
-
-        y_0_4 = down_plain(0, 4, 6, bank=6)
-        y_1_4 = down_plain(1, 4, 6, bank=1)
-        y_0_6 = down_plain(0, 6, E, bank=4)
-        y_1_6 = down_plain(1, 6, E, bank=0)
-        y_2_4 = down_plain(2, 4, E, bank=3)
-
-        for window, width in ((windows[1], T - DMA_CLEARED), (windows[2], T)):
-            nc.scalar.activation(window[:, :width], zero[:, :1].to_broadcast([P, width]), SILU)
-
-        def scatter_times_gate(t, first, last, values):
-            nc.vector.tensor_tensor(windows[t][:].indirect(slots(first, last)), values, gate_of(first, last), MULT)
-
-        def scatter_gated(t, first, last, values):
-            nc.vector.tensor_copy(windows[t][:].indirect(slots(first, last)), values)
-
-        scatter_times_gate(0, 0, 2, y_0_0[:])
-        scatter_gated(1, 0, 2, gated_1_0[:])
-        scatter_gated(2, 0, 2, gated_2_0[:])
-        scatter_gated(0, 2, 4, gated_0_2[:, 0, :])
-        scatter_gated(1, 2, 4, gated_1_2[:, 0, :])
-        scatter_times_gate(2, 2, 4, y_2_2)
-        scatter_times_gate(0, 4, 6, y_0_4)
-        scatter_times_gate(1, 4, 6, y_1_4)
-        scatter_times_gate(0, 6, E, y_0_6)
-        scatter_times_gate(1, 6, E, y_1_6)
-        for t in range(2):
+        def store(t):
             nc.sync.dma_start(out[t * P : (t + 1) * P, :], windows[t][:])
-        scatter_times_gate(2, 4, E, y_2_4)
-        nc.sync.dma_start(out[2 * P :, :], windows[2][:])
+
+        gated_1 = held([P, S], F32, "gated_1")
+        gated_2 = held([P, S], F32, "gated_2")
+
+        for e in range(6):
+            up(e)
+        quantise(0, bank=3, buffer="act_5")
+        up(6)
+        up(7)
+        quantise(2, bank=0, buffer="act_7")
+        quantise(4, bank=1)
+        quantise(6, bank=3)
+        y_2_0 = down_plain(2, 0, 3, bank=2)
+        down_gated(1, 0, 4, 4, gated_1)
+        y_0_4 = down_plain(0, 4, E, bank=0)
+        y_0_0 = down_plain(0, 0, 4, bank=5)
+        scatter_on_vector(2, 0, 3, y_2_0)
+        down_gated(1, 4, E, 6, gated_1)
+        scatter_on_vector(0, 4, E, y_0_4)
+        down_gated(2, 3, 6, 7, gated_2)
+        down_gated(2, 6, E, 1, gated_2)
+        for first in range(0, E, 2):
+            scatter_on_scalar(1, first * C, (first + 2) * C, gated_1)
+        store(1)
+        scatter_on_vector(0, 0, 4, y_0_0)
+        store(0)
+        scatter_on_scalar(2, 384, 704, gated_2)
+        scatter_on_scalar(2, 704, S, gated_2)
+        store(2)

@@ -87,7 +87,7 @@ def tile_moe_pkd_glu_silu_kernel(
         nc.sync.dma_start(x_table[:, C:].bitcast(I32), x_int[:, C:])
         load_plane(w1_scales, 0, E, w1_plane, "w1_plane")
         load_words(w3_words, 0, 2, w3, "w3")
-        load_plane(w3_scales, 0, 4, w3_plane, "w3_plane", on_gpsimd=3)
+        load_plane(w3_scales, 0, 4, w3_plane, "w3_plane")
         load_words(w1_words, 2, 4, w1, "w1")
         load_words(w3_words, 2, 4, w3, "w3")
         load_words(w1_words, 4, 6, w1, "w1")

@@ -79,26 +79,21 @@ def tile_moe_pkd_glu_silu_kernel(
         w1, w3, w2 = {}, {}, {}
         w1_plane, w3_plane, w2_plane = {}, {}, {}
         x_table = held([P, T], U32, "x_table")
-        x_int = x_words[0].rearrange("p t r -> p (t r)").bitcast(I32)
-        nc.scalar.dma_start(x_table[:, :C].bitcast(I32), x_int[:, :C])
-        load_words(w1_words, 0, 2, w1, "w1")
+        load_words(w1_words, 0, 4, w1, "w1")
         nc.sync.dma_start(offsets[:], offs)
         load_scale_rows(x_plane, x_scales.rearrange("o q w -> q o w"))
-        nc.sync.dma_start(x_table[:, C:].bitcast(I32), x_int[:, C:])
+        nc.sync.dma_start(x_table[:].bitcast(I32), x_words[0].rearrange("p t r -> p (t r)").bitcast(I32))
         load_plane(w1_scales, 0, E, w1_plane, "w1_plane")
         load_words(w3_words, 0, 2, w3, "w3")
-        load_plane(w3_scales, 0, 4, w3_plane, "w3_plane")
-        load_words(w1_words, 2, 4, w1, "w1")
-        load_words(w3_words, 2, 4, w3, "w3")
-        load_words(w1_words, 4, 6, w1, "w1")
-        load_plane(w3_scales, 4, 8, w3_plane, "w3_plane")
-        load_words(w3_words, 4, 6, w3, "w3")
-        load_words(w1_words, 6, 8, w1, "w1")
-        load_words(w3_words, 6, 8, w3, "w3")
+        load_plane(w3_scales, 0, E, w3_plane, "w3_plane")
+        for first in (4, 6):
+            load_words(w1_words, first, first + 2, w1, "w1")
+            load_words(w3_words, first - 2, first, w3, "w3")
+        load_words(w3_words, 6, E, w3, "w3")
         load_plane(w2_scales, 0, 8, w2_plane, "w2_plane")
         load_words(w2_words, 0, 4, w2, "w2")
-        load_words(w2_words, 4, 8, w2, "w2")
         load_gate(0, 4)
+        load_words(w2_words, 4, 8, w2, "w2")
         load_gate(4, 8)
 
         ident = held([P, P], F32, "ident")
@@ -108,33 +103,20 @@ def tile_moe_pkd_glu_silu_kernel(
         for window in windows[1:]:
             nc.scalar.activation(window[:], zero[:].to_broadcast([P, T]), SILU)
 
-        xg, h, hq = {}, {}, {}
+        xg, h, ht, hq = {}, {}, {}, {}
         slot_plane = held([P, S], U8, "slot_plane")
         xs = [slot_plane[:, e * C : (e + 1) * C] for e in range(E)]
-        warm_codes = held([P, C], U32, "warm_codes")
-        nc.vector.tensor_copy(warm_codes[:], x_table[:, :C])
-        nc.vector.tensor_copy(slot_plane[:, : 4 * C], x_plane[:].indirect(slots(0, 4)))
-        warm_ps = banked([P, H], "warm_ps", 7)
-        for width in (H, H, 64):
-            nc.tensor.matmul_mx(
-                warm_ps[:, :width],
-                lhsT=warm_codes[:].bitcast(FP8X4),
-                lhsT_scale=xs[0],
-                rhs=w1[0][:, : 2 * width].bitcast(FP4X4),
-                rhs_scale=slot_plane[:, :width],
-                start=True,
-                stop=True,
-            )
-        nc.vector.tensor_copy(slot_plane[:, 4 * C :], x_plane[:].indirect(slots(4, E)))
+        for first, last in ((0, 4), (4, E)):
+            nc.vector.tensor_copy(slot_plane[:, first * C : last * C], x_plane[:].indirect(slots(first, last)))
         for first, last in ((0, 2), (2, 4), (4, E)):
             gathered = held([P, (last - first) * C], U32, f"xg_{first}")
             nc.vector.tensor_copy(gathered[:], x_table[:].indirect(slots(first, last)))
             for e in range(first, last):
                 xg[e] = gathered[:, (e - first) * C : (e - first + 1) * C]
 
-        def up(e):
-            a_ps = banked([P, H], f"a_ps_{e}", e % 3)
-            b_ps = banked([P, H], f"b_ps_{e}", 4 + e % 4)
+        def up(e, a_bank, b_bank):
+            a_ps = banked([P, H], f"a_ps_{e}", a_bank)
+            b_ps = banked([P, H], f"b_ps_{e}", b_bank)
             for acc, words, plane in ((a_ps, w1, w1_plane), (b_ps, w3, w3_plane)):
                 nc.tensor.matmul_mx(
                     acc[:],
@@ -150,21 +132,25 @@ def tile_moe_pkd_glu_silu_kernel(
             h[e] = held([P, 2, P, 2], BF16, f"h_{e}")
             nc.vector.tensor_tensor(h[e][:], b_ps[:].rearrange("s (q u v) -> s u q v", u=2, v=2), act[:], MULT)
 
-        def quantise(first, bank, buffer=None):
-            ht_ps = banked([P, 2, 2, C], f"ht_ps_{first}", bank)
-            for j in range(2):
+        def turn(first, last, bank):
+            count = last - first
+            ht_ps = banked([P, count, 2, C], f"ht_ps_{first}", bank)
+            for j in range(count):
                 pairs = h[first + j][:].rearrange("s u q v -> s (u q v)").bitcast(F32)
                 for u in range(2):
                     nc.tensor.transpose(ht_ps[:, j, u, :], pairs[:, u * P : (u + 1) * P], ident[:])
-            ht = held([P, 2 * C * 4], BF16, f"ht_{first}")
+            ht[first] = held([P, count * C * 4], BF16, f"ht_{first}")
             nc.scalar.copy(
-                ht[:].bitcast(F32).rearrange("q (j s u) -> q j s u", j=2, u=2),
+                ht[first][:].bitcast(F32).rearrange("q (j s u) -> q j s u", j=count, u=2),
                 ht_ps[:].rearrange("q j u s -> q j s u"),
             )
-            codes = held([P, 2 * C], U32, f"h_codes_{first}", buffer)
-            plane = held([P, 2 * C], U8, f"h_plane_{first}")
-            nc.vector.quantize_mx(out=codes[:].bitcast(FP8X4), scales=plane[:], in_=ht[:])
-            for j in range(2):
+
+        def quantise(first, last, buffer=None):
+            count = last - first
+            codes = held([P, count * C], U32, f"h_codes_{first}", buffer)
+            plane = held([P, count * C], U8, f"h_plane_{first}")
+            nc.vector.quantize_mx(out=codes[:].bitcast(FP8X4), scales=plane[:], in_=ht[first][:])
+            for j in range(count):
                 hq[first + j] = (codes[:, j * C : (j + 1) * C], plane[:, j * C : (j + 1) * C])
 
         def down(t, first, last, bank):
@@ -204,23 +190,31 @@ def tile_moe_pkd_glu_silu_kernel(
         gated_2 = held([P, S], F32, "gated_2")
 
         for e in range(6):
-            up(e)
-        quantise(0, bank=3, buffer="act_5")
-        up(6)
-        up(7)
-        quantise(2, bank=0, buffer="act_7")
-        quantise(4, bank=1)
-        quantise(6, bank=3)
-        y_2_0 = down_plain(2, 0, 3, bank=2)
+            up(e, a_bank=e % 3, b_bank=4 + e % 4)
+        up(6, a_bank=0, b_bank=6)
+        turn(0, 2, bank=0)
+        up(7, a_bank=1, b_bank=7)
+        quantise(0, 2)
+        turn(2, 4, bank=2)
+        quantise(2, 4)
+        turn(4, 6, bank=3)
+        quantise(4, 6)
+        turn(6, 7, bank=6)
+        quantise(6, 7)
+        turn(7, E, bank=7)
         down_gated(1, 0, 4, 4, gated_1)
-        y_0_4 = down_plain(0, 4, E, bank=0)
+        y_2_0 = down_plain(2, 0, 3, bank=1)
         y_0_0 = down_plain(0, 0, 4, bank=5)
+        quantise(7, E, buffer="h_codes_0")
+        scatter_on_scalar(1, 0, 2 * C, gated_1)
         scatter_on_vector(2, 0, 3, y_2_0)
-        down_gated(1, 4, E, 6, gated_1)
+        y_0_4 = down_plain(0, 4, E, bank=4)
+        scatter_on_scalar(1, 2 * C, 4 * C, gated_1)
+        down_gated(1, 4, E, 3, gated_1)
         scatter_on_vector(0, 4, E, y_0_4)
-        down_gated(2, 3, 6, 7, gated_2)
-        down_gated(2, 6, E, 1, gated_2)
-        for first in range(0, E, 2):
+        down_gated(2, 3, 6, 2, gated_2)
+        down_gated(2, 6, E, 0, gated_2)
+        for first in (4, 6):
             scatter_on_scalar(1, first * C, (first + 2) * C, gated_1)
         store(1)
         scatter_on_vector(0, 0, 4, y_0_0)

from contextlib import ExitStack

import concourse.mybir as mybir
from concourse.masks import make_identity

K, T, E, C, H, N = 512, 2048, 8, 128, 512, 384
S = E * C
P = 128
FLOPS = 2 * S * (2 * K * H + H * N)

F32 = mybir.dt.float32
BF16 = mybir.dt.bfloat16
I32 = mybir.dt.int32
U32 = mybir.dt.uint32
U16 = mybir.dt.uint16
U8 = mybir.dt.uint8
FP8X4 = mybir.dt.float8_e4m3fn_x4
FP4X4 = mybir.dt.float4_e2m1fn_x4
MULT = mybir.AluOpType.mult
SILU = mybir.ActivationFunctionType.Silu
COPY = mybir.ActivationFunctionType.Copy


def tile_moe_pkd_glu_silu_kernel(
    tc, x_words, x_scales, w1_words, w1_scales, w3_words, w3_scales, w2_words, w2_scales, gate, offs, out
):
    nc = tc.nc
    with ExitStack() as ctx:
        keep = ctx.enter_context(tc.tile_pool(name="keep", bufs=1))
        psum = ctx.enter_context(tc.psum_pool(name="psum", bufs=1))

        def held(shape, dtype, name, buffer=None):
            return keep.tile(shape, dtype, name=name, tag=buffer or name, align_bytes=64)

        def banked(shape, name, bank):
            return psum.tile(shape, F32, name=name, tag=f"bank_{bank}")

        offsets = keep.tile([P, S // 16], U16, name="offsets")

        def slots(first, last):
            return offsets[:, first * C // 16 : last * C // 16]

        def load_scale_rows(plane, scales, on_gpsimd=0):
            by_row = scales.rearrange("(q r) e w -> r q e w", r=4)
            as_int = plane[:].bitcast(I32)
            for r in range(4):
                queue = nc.gpsimd if r >= 4 - on_gpsimd else nc.sync
                queue.dma_start(
                    as_int[r:P:32, :].rearrange("q (e w) -> q e w", e=scales.shape[1]), by_row[r].bitcast(I32)
                )

        def load_plane(scales, first, last, planes, name, on_gpsimd=0, buffer=None):
            width = scales.shape[3]
            plane = held([P, (last - first) * width], U8, f"{name}_{first}", buffer)
            load_scale_rows(plane, scales[first:last].rearrange("e s q w -> q (e s) w"), on_gpsimd)
            for e in range(first, last):
                planes[e] = plane[:, (e - first) * width : (e - first + 1) * width]

        def load_words(words, first, last, into, name):
            tile = held([P, last - first, words.shape[3]], U8, f"{name}_{first}")
            nc.sync.dma_start(tile[:].bitcast(I32), words[first:last, 0].rearrange("e p w -> p e w").bitcast(I32))
            for e in range(first, last):
                into[e] = tile[:, e - first, :]

        gates = held([P, S], F32, "gates")

        def load_gate(first, last):
            nc.sync.dma_start(gates[:, first * C : last * C], gate[:P, first * C : last * C])

        def gate_of(first, last):
            return gates[:, first * C : last * C]

        x_plane = held([P, T], U8, "x_plane")
        nc.vector.memset(x_plane[:].bitcast(I32), 0)
        zero = held([P, 1], F32, "zero")
        nc.vector.memset(zero[:], 0.0)
        windows = [keep.tile([P, T], F32, name=f"window_{t}") for t in range(N // P)]

        w1, w3, w2 = {}, {}, {}
        w1_plane, w3_plane, w2_plane = {}, {}, {}
        x_table = held([P, T], U32, "x_table")
        load_words(w1_words, 0, 4, w1, "w1")
        nc.sync.dma_start(offsets[:], offs)
        load_scale_rows(x_plane, x_scales.rearrange("o q w -> q o w"))
        nc.sync.dma_start(x_table[:].bitcast(I32), x_words[0].rearrange("p t r -> p (t r)").bitcast(I32))
        load_plane(w1_scales, 0, E, w1_plane, "w1_plane")
        load_words(w3_words, 0, 2, w3, "w3")
        load_plane(w3_scales, 0, E, w3_plane, "w3_plane")
        for first in (4, 6):
            load_words(w1_words, first, first + 2, w1, "w1")
            load_words(w3_words, first - 2, first, w3, "w3")
        load_words(w3_words, 6, E, w3, "w3")
        load_plane(w2_scales, 0, 8, w2_plane, "w2_plane")
        load_words(w2_words, 0, 4, w2, "w2")
        load_gate(0, 4)
        load_words(w2_words, 4, 8, w2, "w2")
        load_gate(4, 8)

        ident = held([P, P], F32, "ident")
        make_identity(nc, ident[:])

        nc.vector.memset(windows[0][:], 0.0)
        for window in windows[1:]:
            nc.scalar.activation(window[:], zero[:].to_broadcast([P, T]), SILU)

        xg, h, ht, hq = {}, {}, {}, {}
        slot_plane = held([P, S], U8, "slot_plane")
        xs = [slot_plane[:, e * C : (e + 1) * C] for e in range(E)]
        for first, last in ((0, 4), (4, E)):
            nc.vector.tensor_copy(slot_plane[:, first * C : last * C], x_plane[:].indirect(slots(first, last)))
        for first, last in ((0, 2), (2, 4), (4, E)):
            gathered = held([P, (last - first) * C], U32, f"xg_{first}")
            nc.vector.tensor_copy(gathered[:], x_table[:].indirect(slots(first, last)))
            for e in range(first, last):
                xg[e] = gathered[:, (e - first) * C : (e - first + 1) * C]

        def up(e, a_bank, b_bank):
            a_ps = banked([P, H], f"a_ps_{e}", a_bank)
            b_ps = banked([P, H], f"b_ps_{e}", b_bank)
            for acc, words, plane in ((a_ps, w1, w1_plane), (b_ps, w3, w3_plane)):
                nc.tensor.matmul_mx(
                    acc[:],
                    lhsT=xg[e].bitcast(FP8X4),
                    lhsT_scale=xs[e],
                    rhs=words[e].bitcast(FP4X4),
                    rhs_scale=plane[e],
                    start=True,
                    stop=True,
                )
            act = held([P, 2, P, 2], F32, f"act_{e}")
            nc.scalar.activation(act[:], a_ps[:].rearrange("s (q u v) -> s u q v", u=2, v=2), SILU)
            h[e] = held([P, 2, P, 2], BF16, f"h_{e}")
            nc.vector.tensor_tensor(h[e][:], b_ps[:].rearrange("s (q u v) -> s u q v", u=2, v=2), act[:], MULT)

        def turn(first, last, bank):
            count = last - first
            ht_ps = banked([P, count, 2, C], f"ht_ps_{first}", bank)
            for j in range(count):
                pairs = h[first + j][:].rearrange("s u q v -> s (u q v)").bitcast(F32)
                for u in range(2):
                    nc.tensor.transpose(ht_ps[:, j, u, :], pairs[:, u * P : (u + 1) * P], ident[:])
            ht[first] = held([P, count * C * 4], BF16, f"ht_{first}")
            nc.scalar.copy(
                ht[first][:].bitcast(F32).rearrange("q (j s u) -> q j s u", j=count, u=2),
                ht_ps[:].rearrange("q j u s -> q j s u"),
            )

        def quantise(first, last, buffer=None):
            count = last - first
            codes = held([P, count * C], U32, f"h_codes_{first}", buffer)
            plane = held([P, count * C], U8, f"h_plane_{first}")
            nc.vector.quantize_mx(out=codes[:].bitcast(FP8X4), scales=plane[:], in_=ht[first][:])
            for j in range(count):
                hq[first + j] = (codes[:, j * C : (j + 1) * C], plane[:, j * C : (j + 1) * C])

        def down(t, first, last, bank):
            y_ps = banked([P, (last - first) * C], f"y_ps_{t}_{first}", bank)
            for e in range(first, last):
                nc.tensor.matmul_mx(
                    y_ps[:, (e - first) * C : (e - first + 1) * C],
                    lhsT=w2[e][:, 2 * t * P : 2 * (t + 1) * P].bitcast(FP4X4),
                    lhsT_scale=w2_plane[e][:, t * P : (t + 1) * P],
                    rhs=hq[e][0].bitcast(FP8X4),
                    rhs_scale=hq[e][1],
                    start=True,
                    stop=True,
                )
            return y_ps

        def down_plain(t, first, last, bank, buffer=None):
            y_ps = down(t, first, last, bank)
            y_sb = held([P, (last - first) * C], F32, f"y_{t}_{first}", buffer)
            nc.scalar.copy(y_sb[:], y_ps[:])
            return y_sb

        def down_gated(t, first, last, bank, into):
            y_ps = down(t, first, last, bank)
            nc.vector.tensor_tensor(into[:, first * C : last * C], y_ps[:], gate_of(first, last), MULT)

        def scatter_on_vector(t, first, last, values):
            nc.vector.tensor_tensor(windows[t][:].indirect(slots(first, last)), values[:], gate_of(first, last), MULT)

        def scatter_on_scalar(t, first, last, gated):
            nc.scalar.activation(windows[t][:].indirect(offsets[:, first // 16 : last // 16]), gated[:, first:last], COPY)

        def store(t):
            nc.sync.dma_start(out[t * P : (t + 1) * P, :], windows[t][:])

        gated_1 = held([P, S], F32, "gated_1")
        gated_2 = held([P, S], F32, "gated_2")

        for e in range(6):
            up(e, a_bank=e % 3, b_bank=4 + e % 4)
        up(6, a_bank=0, b_bank=6)
        turn(0, 2, bank=0)
        up(7, a_bank=1, b_bank=7)
        quantise(0, 2)
        turn(2, 4, bank=2)
        quantise(2, 4)
        turn(4, 6, bank=3)
        quantise(4, 6)
        turn(6, 7, bank=6)
        quantise(6, 7)
        turn(7, E, bank=7)
        down_gated(1, 0, 4, 4, gated_1)
        y_2_0 = down_plain(2, 0, 3, bank=1)
        y_0_0 = down_plain(0, 0, 4, bank=5)
        quantise(7, E, buffer="h_codes_0")
        scatter_on_scalar(1, 0, 2 * C, gated_1)
        scatter_on_vector(2, 0, 3, y_2_0)
        y_0_4 = down_plain(0, 4, E, bank=4)
        scatter_on_scalar(1, 2 * C, 4 * C, gated_1)
        down_gated(1, 4, E, 3, gated_1)
        scatter_on_vector(0, 4, E, y_0_4)
        down_gated(2, 3, 6, 2, gated_2)
        down_gated(2, 6, E, 0, gated_2)
        for first in (4, 6):
            scatter_on_scalar(1, first * C, (first + 2) * C, gated_1)
        store(1)
        scatter_on_vector(0, 0, 4, y_0_0)
        store(0)
        scatter_on_scalar(2, 384, 704, gated_2)
        scatter_on_scalar(2, 704, S, gated_2)
        store(2)
